import numpy as np, ml_dtypes
CORES = [23,119,17,113]
N = 4
BF = ml_dtypes.bfloat16
def gentries(a):
    return np.ascontiguousarray(a.reshape(8, 16, -1).transpose(0, 2, 1)).reshape(8, -1)
def gtable(e):
    e = np.asarray(e); return np.ascontiguousarray(e.reshape(8, -1, 16).transpose(0, 2, 1)).reshape(128, -1).astype(np.int32)
W, S, ST, HOP = 4608, 256, 3, 1
def sig(v):
    return np.minimum(np.floor(v), 32640).astype(np.float32).astype(BF)
def parts(rng):
    sc = np.exp2(rng.integers(9, 16, (N, 8, 16, 1)).astype(np.float64))
    x = rng.random((N, 8, 16, W)) * sc
    t = np.floor(np.add.reduce(sc, axis=2)[:, :, None, :] * (0.15 + 0.2 * rng.random((N, 8, 16, 1))))
    o = np.argsort(rng.random((N, 8, S)), axis=-1)
    b = np.take_along_axis(o, np.floor(S * rng.random((N, 8, W)) ** 2).astype(np.int64), 2)
    nbr = rng.integers(0, W, (N, 8, 16, W)); L = rng.integers(0, W, (N, 8, S, 16))
    return x, t, b, nbr, L
def plant(rng, b, L):
    n = S // 8
    for q in range(N):
        for g in range(8):
            o = rng.permutation(S); pos = rng.permutation(W)[:3 * n].reshape(n, 3); b[q, g, pos] = o[:n, None]
            rows = np.argsort(rng.random((n, 16)), axis=1)[:, :6]
            L[q, g, o[:n, None], rows] = np.take_along_axis(pos, rng.integers(0, 3, (n, 6)), 1)
            rows = np.argsort(rng.random((n, 16)), axis=1)[:, :6]
            L[q, g, o[n:2 * n, None], rows] = np.take_along_axis(pos[rng.integers(0, n, n)], rng.integers(0, 3, (n, 6)), 1)
            L[q, g, o[2 * n]] = L[q, g, o[2 * n + 1]]; L[q, g, o[2 * n + 2]] = L[q, g, o[2 * n + 3]]
def pack(x, t, b, nbr, L):
    return {"tr": np.stack([gtable(a.reshape(8, -1)) for a in L]), "xs": np.ascontiguousarray(sig(x).reshape(N, 128, W)), "nb": np.ascontiguousarray(nbr.reshape(N, 128, W)).astype(np.int32),
            "lb": np.ascontiguousarray(b).astype(np.int32), "th": np.ascontiguousarray(t.reshape(N, 128, 1)).astype(np.int32)}
def setup_inputs(rng):
    x, t, b, nbr, L = parts(rng); plant(rng, b, L)
    return pack(x, t, b, nbr, L)
def setup_inputs_ties(rng):
    x, t, b, nbr, L = parts(rng)
    unit = rng.choice(np.array([1, 2, 64, 4096]), (N, 8, 1, 1)); unit[:, ::2] = 1
    x = unit * rng.integers(0, 3, (N, 8, 16, W)); x[:, 3] = 0
    t = unit * rng.integers(9, 17, (N, 8, 16, 1))
    b = rng.choice(np.array([0, 1, S // 2, S - 1]), (N, 8, W)); b[:, 1] = rng.integers(0, 24, (N, W)); b[:, 4] = rng.integers(S - 9, S, (N, W))
    return pack(x, t, b, nbr, L)
def setup_inputs_alike(rng):
    x, t, b, nbr, L = parts(rng)
    L[:, 0] = L[:, 0, :1].copy(); L[:, 1] = L[:, 1, :, :1].copy()
    b[:, 2] = 0; b[:, 3] = S - 1
    L[:, 4] = rng.choice(np.array([0, W - 1]), (N, S, 16)); nbr[:, 4] = rng.choice(np.array([0, W - 1, W // 2, 1]), (N, 16, W))
    L[:, 5] = rng.integers(W - 20, W, (N, S, 16))
    for g in (6, 7): L[:, g] = np.arange(S)[None, :, None] + S * rng.integers(0, W // S, (N, S, 16))
    b[:, 6] = np.arange(W) % S; b[:, 7] = (np.arange(W) % S + 1) % S
    return pack(x, t, b, nbr, L)
def setup_inputs_bounds(rng):
    x, t, b, nbr, L = parts(rng); plant(rng, b, L)
    t = np.where(rng.random((N, 8, 16, 1)) < 0.5, rng.choice(np.array([0, 524287]), (N, 8, 16, 1)), t); t[0] = 0; t[1] = 524287
    share = rng.choice(np.array([0.06, 0.3, 0.5, 0.94]), (N, 4, 1, 1))
    x[:, ::2] = np.where(rng.random((N, 4, 16, W)) < share, 32640, 0)
    return pack(x, t, b, nbr, L)
def setup_inputs_far(rng):
    x, t, b, nbr, L = parts(rng); plant(rng, b, L); i = np.arange(S); v = np.arange(W); m = W // S - 1
    low = rng.integers(0, 16, (N, 8, 16, W))
    for g, share in ((0, 0.5), (6, 0.4)):
        x[:, g] = np.where(rng.random((N, 16, W)) < share, 32640, low[:, g]); t[:, g] = rng.integers(200000, 320000, (N, 16, 1))
    for g, n in ((1, 1), (7, 2)):
        x[:, g] = np.where(np.argsort(rng.random((N, 16, W)), axis=1) < n, low[:, g], 32640); t[:, g] = rng.integers(0, 2 ** 17, (N, 16, 1))
    for g in (2, 4, 5):
        L[:, g] = i[None, :, None] + S * rng.integers(0, m, (N, S, 16)); b[:, g] = (v % S + 1) % S
    x[:, 2] = np.where(v < m * S, low[:, 2], 32640)
    np.put_along_axis(L[:, 2], rng.integers(0, 16, (N, S, 1)), i[None, :, None] + m * S, 2)
    t[:, 2] = np.where(rng.random((N, 16, 1)) < 0.5, rng.integers(0, 3, (N, 16, 1)), rng.integers(0, 522241, (N, 16, 1)))
    t[:, 2, 0::4] = rng.integers(393216, 489000, (N, 4, 1)); t[:, 2, 2::4] = rng.integers(327680, 393216, (N, 4, 1))
    t[:, 3] = rng.integers(0, 3, (N, 16, 1)); t[:, 3, ::2] = 0
    a = np.argsort(rng.random((N, W)), axis=1)[:, :S // 2]; L[:, 3, :S // 2] = a[:, :, None]
    np.put_along_axis(b[:, 3], a, (S // 2 + i[:S // 2])[None, :], 1)
    t[:, 4] = rng.integers(0, 3, (N, 16, 1))
    x[:, 5] = np.where(v < m * S, np.where(rng.random((N, 16, W)) < 0.5, 32640, low[:, 5]), rng.integers(15000, 17500, (N, 16, W)))
    nbr[:, 5] = rng.integers(m * S, W, (N, 16, W)); t[:, 5] = rng.integers(489600, 524288, (N, 16, 1))
    return pack(x, t, b, nbr, L)
def setup_inputs_spread(rng):
    x, t, b, nbr, L = parts(rng)
    x = rng.random((N, 8, 16, W)) * np.exp2(15 * rng.random((N, 8, 1, W))) * (rng.random((N, 8, 1, W)) > 0.0625)
    t = np.minimum(np.floor(np.exp2(10 + 9 * rng.random((N, 8, 16, 1)))), 524287)
    b = np.minimum(np.floor(S * rng.random((N, 8, W)) ** 4).astype(np.int64), S - 1)
    L = np.minimum(np.floor(W * rng.random((N, 8, S, 16)) ** 2).astype(np.int64), W - 1)
    plant(rng, b, L)
    return pack(x, t, b, nbr, L)
def check_inputs(d):
    bad = []; v = np.asarray(d["xs"]).astype(np.float32)
    if not (np.all(v == np.floor(v)) and np.min(v) >= 0 and np.max(v) <= 32640): bad.append("whole numbers and range of xs")
    for k, hi in (("tr", W - 1), ("nb", W - 1), ("lb", S - 1), ("th", 524287)):
        if np.min(d[k]) < 0 or np.max(d[k]) > hi: bad.append("range of " + k)
    return bad
def pick(X, c):
    return np.take_along_axis(X, c.reshape(N, 8, 1, S * 16), 3).reshape(N, 8, 16, S, 16)
def reference(tr, xs, nb, lb, th):
    X = xs.astype(np.float32).astype(np.int64).reshape(N, 8, 16, W); near = nb.astype(np.int64).reshape(N, 8, 16, W)
    t = th.astype(np.int64).reshape(N, 8, 1, 16); b = lb.astype(np.int64); i = np.arange(S)
    L = np.stack([gentries(a) for a in tr]).astype(np.int64).reshape(N, 8, S, 16)
    for st in range(ST):
        x = pick(X, L); y = np.add.reduce(x, axis=4) >> 4
        E = np.add.reduce(np.abs(x - y[..., None]), axis=2)
        p = np.take_along_axis(L, np.argmin(E, axis=3)[..., None], 3)[..., 0]
        v = np.take_along_axis(b, L.reshape(N, 8, S * 16), 2).reshape(N, 8, S, 16)
        votes = np.add.reduce((v[..., :, None] == v[..., None, :]).astype(np.int64), axis=4)
        H = np.take_along_axis(v, np.argmax(votes, axis=3)[..., None], 3)[..., 0]
        child = (H[..., :, None] == i) & (i[:, None] != i)
        don = np.min(np.where(child, i[:, None], S), axis=2); d0 = np.minimum(don, S - 1)[..., None]
        Ld = np.take_along_axis(L, d0, 2); Ed = np.take_along_axis(E, d0, 2)
        fill = np.take_along_axis(near, p[:, :, None, :], 3).swapaxes(2, 3)
        c = np.where((don < S)[..., None] & (Ed > t), Ld, fill)
        F = np.add.reduce(np.abs(pick(X, c) - y[..., None]), axis=2)
        new = np.where(F < E, c, L)
        again = np.argmax(p[..., :, None] == p[..., None, :], axis=3) < i
        new = np.where(again[..., None], fill, new)
        bb = np.concatenate([b, np.zeros((N, 8, 1), np.int64)], axis=2)
        np.put_along_axis(bb, np.where(again, W, p), np.broadcast_to(i, (N, 8, S)), 2); b = bb[..., :W]
        L = np.roll(new, HOP, axis=0) if st < ST - 1 else new
    return {"yl": np.stack([gtable(a.reshape(8, -1)) for a in L]).astype(np.float32), "yb": np.ascontiguousarray(b).astype(np.float32)}

@@ -1,0 +1,373 @@
+from concourse.mybir import AluOpType, ActivationFunctionType
+
+W, S, ST, HOP = 4608, 256, 3, 1
+TRASH = W
+DON0 = W + 16
+WN = DON0 + ST * (S + 16)
+MAGIC = 12582912.0
+B23, B24 = 8388608.0, 16777216.0
+ISC = {"one": 1.0, "s16": 0.0625, "p8192": 8192.0, "p4608": 4608.0, "n4608": -4608.0, "n2304": -2304.0,
+       "p4096": 4096.0, "neg": -1.0, "nB": -B23, "n32": -32.0}
+ISN = list(ISC)
+SCRATCH = {}
+for _dt, _list in (
+    ("float32", "win:%d lbf:288 thn:128 Lf0:256 Lf1:256 Lf2:256 nw0:256 nw1:256 nw2:256 M:4096 ysb:256 SM:256 tc:256 PW:256 "
+                "QS:256 KB:256 KS:256 SM2:256 pd:16 CD:256 CP:256 t2:256 VAL:16x32 ONE:128 IF:128 BO:128 BT:128 WY:128 B8:16 W8f:24 "
+                "JR:256 BC:16 cf:48 tg:24" % WN),
+    ("bfloat16", "xw:%d X:4096 V:4096 GE:256 EP:256 SB:256 EH:8x16 U:256 NA:256 vs:256 TK:256 VS:16x24 EQ:128x16 HD:256 e5:16 HW:16 "
+                 "IS:%d W8b:32 RR:256 DM:256 TRI:128 RST:128 RA:128 RB:128 RT:128 RM:256 KC2:16x16 N75:128 CT:256 JW:16 ROT:1024 CR:1024"
+                 % (2 * W, 128 * len(ISC))),
+    ("int32", "nbw:%d lbs:288 tri:256 thi:128 HI:16 HJ:16 ci:48 cj:8" % W),
+    ("uint16", "Lu:256 cu:256 pu:16 OFF:32 cw:48"),
+):
+    for _e in _list.split():
+        SCRATCH[_e.split(":")[0]] = ("sbuf", [128] + [int(_x) for _x in _e.split(":")[1].split("x")], _dt)
+BANKS = ("Y0", "Y1", "K0", "K1", "P0", "P1", "VC", "K2")
+for _b in BANKS: SCRATCH[_b] = ("psum", [128, 32, 16] if _b in ("VC", "K2") else [128, 512], "float32")
+SEMAPHORES = (["cv", "ca", "cp", "cg", "sent", "d_lb", "d_tr", "d_th", "d_xa", "d_xb", "d_nb", "d_lab", "d_yb", "d_y0", "d_y1"]
+              + ["r%d%d" % (t, h) for t in range(1, ST) for h in range(2)])
+A, F = AluOpType, ActivationFunctionType
+CFG = {"q": 64, "z": 1152, "gath": 1.55, "scat": 3.5, "fix": 55.0, "pe": 0.5, "link": 3600.0, "slack": [50.0],
+       "pat": "aavavavavaaa" "vavavaaavaaa" "vaavvaaavaaa",
+       "bo": {"cg": 90, "cw": 15, "fi1": 45, "N1": -60, "N0": 10, "XLu1": 15, "pr1": -5, "ys1": 5, "lu1": -15, "vc": -5, "dd0": 15,
+              "ys0": 30, "un1": -5, "mi1": 10, "un0": -30, "c": 90, "Xcu0": 20, "XLu0": 30, "sc0": -5, "mi0": -15, "lu0": 20,
+              "cr": -15, "cv": -60, "co0": 20, "ct": -5, "cc": 20, "sc1": 30, "eq": 90, "ho": 5, "VLu1": -5, "fi0": 20,
+              "VLu0": -5, "dd1": -60}}
+ORDER = {}
+
+
+def banks_of(o): return set(x.split(".")[0] for x in o["r"] + o["w"] if x.split(".")[0] in BANKS)
+
+
+def follow(ops, tensor_in_order):
+    pre = [set() for _ in ops]; lastw, readers, bank = {}, {}, {}
+    for i, o in enumerate(ops):
+        for k in o["r"] + o["w"]:
+            if k in lastw: pre[i].add(lastw[k])
+        for k in o["w"]: pre[i].update(readers.get(k, []))
+        for k in banks_of(o):
+            for e2, j in bank.setdefault(k, {}).items():
+                if e2 != o["e"] or e2 == "p": pre[i].add(j)
+            bank[k][o["e"]] = i
+        if tensor_in_order and o["e"] == "p": pre[i] = set(j for j in pre[i] if ops[j]["e"] != "p")
+        for k in o["r"]: readers.setdefault(k, []).append(i)
+        for k in o["w"]:
+            lastw[k] = i; readers[k] = []
+    return pre
+
+
+def graph(ops):
+    pre = follow(ops, False); sent, soft = {}, set()
+    for i, o in enumerate(ops):
+        if o["e"] == "s":
+            if "s" in sent: pre[i].add(sent["s"]); soft.add((sent["s"], i))
+            sent["s"] = i
+        if o["k"] == "r": sent[o["sem"]] = i
+        if o["k"] == "x": pre[i].add(sent[o["sem"]])
+    suc = [[] for _ in ops]
+    for i in range(len(ops)):
+        for j in pre[i]: suc[j].append(i)
+    return pre, suc, soft
+
+
+def arrange(ops, gr=None):
+    pre, suc, soft = gr or graph(ops); n = len(ops); slack = CFG["slack"][0]
+    lv = [0.0] * n
+    for i in range(n - 1, -1, -1): lv[i] = ops[i]["c"] + ops[i]["lat"] + 60.0 + max([lv[j] for j in suc[i]] + [0.0])
+    lv = [v + 100.0 * CFG["bo"].get(o["t"], 0) for v, o in zip(lv, ops)]
+    free = {e: 0.0 for e in "vapgsx"}; at = [0.0] * n; left = [len(p) for p in pre]
+    ready = [i for i in range(n) if not left[i]]; order = []; end = 0.0; dma = 0.0
+    while ready:
+        t0, e = min((max(at[i], free[ops[i]["e"]]), ops[i]["e"]) for i in ready)
+        i = max((i for i in ready if e == ops[i]["e"] and at[i] <= t0 + slack), key=lambda i: lv[i])
+        o = ops[i]; free[e] = max(at[i], free[e]) + o["c"]; done = free[e] + o["lat"]
+        if o["k"] == "d":
+            dma = max(dma, free[e] + 1200.0) + o["lat"]; done = dma + 800.0
+        order.append(i); ready.remove(i); end = max(end, done)
+        for j in suc[i]:
+            at[j] = max(at[j], free[e] if (i, j) in soft else done + (0.0 if e == "p" and ops[j]["e"] == "p" else 60.0)); left[j] -= 1
+            if not left[j]: ready.append(j)
+    return end, order
+
+
+def emit(g, T, ops):
+    Q = {"v": g.vector, "a": g.scalar, "p": g.tensor, "g": g, "s": g.sync}
+    deps = follow(ops, True)
+    need = set(j for d in deps for j in d)
+    tick, n = {}, {}
+    for i, o in enumerate(ops):
+        if o["k"] == "c" and i in need:
+            n[o["e"]] = n.get(o["e"], 0) + 1; tick[i] = ("c" + o["e"], n[o["e"]])
+        elif o["k"] in ("d", "x"): tick[i] = (o["sem"], o["n"])
+    know = {e: {} for e in Q}; snap = {}
+    for i, o in enumerate(ops):
+        e = o["e"]
+        if o["k"] == "x":
+            snap[i] = {}; continue
+        kn = know[e]; want = {}
+        for j in deps[i]:
+            s, v = tick[j]
+            if want.get(s, (0, 0))[0] < v: want[s] = (v, j)
+        for s, (v, j) in sorted(want.items(), key=lambda z: -z[1][1]):
+            if kn.get(s, 0) < v:
+                Q[e].wait_ge(T.sem[s], v); kn[s] = v
+                for s2, v2 in snap[j].items(): kn[s2] = max(kn.get(s2, 0), v2)
+        snap[i] = dict(kn)
+        ins = o["f"](Q[e], e)
+        if o["k"] == "d": ins.then_inc(T.sem[o["sem"]], 16)
+        elif o["k"] == "c" and i in tick: ins.then_inc(T.sem[tick[i][0]], 1)
+    top = {}
+    for s, v in tick.values(): top[s] = max(top.get(s, 0), v)
+    g.wait_ge(T.sem.sent, sum(o["n"] for o in ops if o["k"] == "r"))
+    for s, v in top.items():
+        if max(kn.get(s, 0) for kn in know.values()) < v: g.sync.wait_ge(T.sem[s], v)
+
+
+def rank_program(g, core, T, topo):
+    rank = T.rank_of(core)
+    if rank is None:
+        return
+    nr = len(T.cores)
+    nxt, prv = T.cores[(rank + HOP) % nr], T.cores[(rank - HOP) % nr]
+    tag = ["c"]; ops = []; FX, GA, PE = CFG["fix"], CFG["gath"], CFG["pe"]
+
+    def op(e, f, c, r, w, k="c", sem=None, n=0, lat=0.0):
+        ops.append({"e": e, "f": f, "c": c, "r": r.split(), "w": w.split(), "k": k, "sem": sem, "n": n, "lat": lat, "t": tag[0]})
+    def dma(e, sem, out, in_, nb, r, w): op(e, lambda q, e: q.dma_start(out, in_), 60.0, r, w, "d", sem, 16, nb / 250.0)
+    def mm(out, l, rh, st, sp, n, r, w): op("p", lambda q, e: q.matmul(out, l, rh, st, sp), n * PE + 5, r, w)
+    def cp(out, in_, n, r, w): op("v", lambda q, e: q.tensor_copy(out, in_), FX + n, r, w)
+    def tt(out, a, b, o, n, r, w): op("v", lambda q, e: q.tensor_tensor(out, a, b, o), FX + n, r, w)
+    def ts(out, a, s1, o0, n, r, w, s2=None, o1=None):
+        if o1 is None: op("v", lambda q, e: q.tensor_scalar(out, a, s1, None, o0), FX + n, r, w)
+        else: op("v", lambda q, e: q.tensor_scalar(out, a, s1, s2, o0, o1), FX + n, r, w)
+    def scan(out, d0, d1, o0, o1, n, r, w): op("v", lambda q, e: q.tensor_tensor_scan(out, d0, d1, 0.0, o0, o1), FX + n, r, w)
+    def ms(ap, c, n, w): op("v", lambda q, e: q.memset(ap, c), FX + n, "", w)
+    def act(out, in_, fn, n, r, w, bias=None, scale=1.0, col=None):
+        if bias is not None: col, r = T.BC[:, bias:bias + 1], r + " BC%d" % bias
+        if col is None: op("a", lambda q, e: q.activation(out, in_, fn, scale=scale), FX + n, r, w)
+        else: op("a", lambda q, e: q.activation(out, in_, fn, bias=col, scale=scale), FX + n, r, w)
+    def iota(out, pat, base, cm, n, w, fl=True):
+        if fl: op("g", lambda q, e: q.iota(out, pat, base, cm, allow_small_or_imprecise_dtypes=True), 130.0 + 2 * n, "", w)
+        else: op("g", lambda q, e: q.iota(out, pat, base, cm), 130.0 + 2 * n, "", w)
+    def sel(out, in_, pat, cmp, fill, base, cm, n, r, w): op("g", lambda q, e: q.affine_select(out, in_, pat, cmp, fill, base, cm), 170.0 + 2 * n, r, w)
+    def I(name):
+        j = ISN.index(name); return T.IS[:, 128 * j:128 * j + 128]
+
+    H = [slice(0, 128), slice(128, 256)]
+    Yb, Kb, Pb = [T.Y0, T.Y1], [T.K0, T.K1], [T.P0, T.P1]
+    rcol = T.cf[:, 40:41]; NQ = 128 // CFG["q"]; Z = CFG["z"]
+
+    dma("s", "d_lb", T.lbs[:], T.lb[:], 32 * W, "", "lbs")
+    dma("s", "d_tr", T.tri[:], T.tr[:], 131072, "", "tri")
+    dma("s", "d_th", T.thi[0:1, :], T.th[:], 512, "", "thi")
+    dma("s", "d_xa", T.xw[:, 0:W], T.xs[:], 256 * W, "", "xa")
+    iota(T.ONE[:], [[0, 128]], 1, 0, 128, "ONE")
+    ms(T.win[:, 0:Z], 0.0, Z, "z0"); ms(T.win[:, Z:W - 2 * Z], 0.0, W - 3 * Z, "z1")
+    for j in (2, 1): act(T.win[:, W - j * Z:W - j * Z + Z], T.win[:, 0:Z], F.Copy, Z, "z0", "z%d" % (j + 1))
+    cp(T.lbf[:], T.lbs[:], 288, "lbs", "lbf")
+    dma("s", "d_lab", T.win[0:128:16, 0:W], T.lbf[:], 32 * W, "lbf", "lab z0 z1 z2 z3")
+    dma("s", "d_nb", T.nbw[:], T.nb[:], 512 * W, "lab", "nbw")
+    dma("s", "d_xb", T.xw[:, W:2 * W], T.xs[:], 256 * W, "lab", "xb")
+    tag[0] = "cg"
+    sel(T.IF[:], T.ONE[:], [[-1, 128]], A.is_equal, 0.0, 0, 1, 128, "ONE", "IF")
+    sel(T.B8[:, 8:16], T.ONE[:, 0:8], [[-16, 8]], A.is_ge, 0.0, 0, 1, 8, "ONE", "B8t")
+    sel(T.B8[:, 0:8], T.B8[:, 8:16], [[16, 8]], A.is_ge, 0.0, 15, -1, 8, "B8t", "B8")
+    sel(T.W8f[:, 16:24], T.ONE[:, 0:8], [[-16, 8]], A.is_equal, 0.0, 0, 1, 8, "ONE", "Wself")
+    sel(T.BT[:], T.ONE[:], [[-16, 8], [0, 16]], A.is_ge, 0.0, 0, 1, 128, "ONE", "BT")
+    sel(T.BO[:], T.BT[:], [[16, 8], [0, 16]], A.is_ge, 0.0, 15, -1, 128, "BT", "BO")
+    iota(T.RR[:], [[0, 16], [1, 16]], 0, 0, 256, "RR")
+    iota(T.ci[:, 0:16], [[16, 16]], 15, 0, 16, "ci0", False)
+    iota(T.ci[:, 16:32], [[1, 16]], 0, 0, 16, "ci1", False)
+    iota(T.ci[:, 32:48], [[0, 16]], 0, 1, 16, "ci2", False)
+    iota(T.KC2[:], [[0, 16], [-256, 16]], 3840, 0, 256, "KC2")
+    iota(T.JR[:], [[1, 256]], 0, 0, 256, "JR")
+    tag[0] = "cr"
+    iota(T.ROT[:], [[0, 1024]], 0, 0, 1024, "ROT")
+    for pat, cmp, fill, base, cm in (([[1, 8], [1, 128]], A.not_equal, 1.0, 1, -1), ([[1, 8], [1, 128]], A.not_equal, 1.0, -15, -1),
+                                     ([[0, 8], [1, 128]], A.not_equal, -1.0, 0, -1), ([[0, 8], [-16, 8], [0, 16]], A.is_ge, 0.0, 0, 1),
+                                     ([[0, 8], [16, 8], [0, 16]], A.is_ge, 0.0, 15, -1)):
+        sel(T.ROT[:], T.ROT[:], pat, cmp, fill, base, cm, 1024, "ROT", "ROT")
+    iota(T.VAL[:], [[16, 16], [1, 32]], 0, 0, 512, "VALp0 VALp1 VALj")
+    iota(T.win[:, W:WN], [[0, WN - W]], 0, 0, WN - W, "don")
+    tag[0] = "ca"
+    for nm in ISN: act(I(nm), T.IF[:], F.Copy, 128, "IF", "I" + nm, scale=ISC[nm])
+    for j, c in enumerate((-16.0, 16.0, 1.0)): act(T.W8b[:, 8 * j:8 * j + 8], T.B8[:, 0:8], F.Copy, 64, "B8", "W8b%d" % j, scale=c)
+    act(T.W8b[:, 24:32], T.W8f[:, 16:24], F.Copy, 64, "Wself", "W8b3")
+    for j, c in enumerate((32.0, -32.0)): act(T.W8f[:, 8 * j:8 * j + 8], T.B8[:, 0:8], F.Copy, 64, "B8", "W8f%d" % j, scale=c)
+    act(T.WY[:], T.BO[:], F.Copy, 128, "BO", "WY", scale=-16.0)
+    tag[0] = "cv"
+    cp(T.Lu[:], T.tri[:], 256, "tri", "Lu0 Lu1")
+    ms(T.N75[:], -7.5, 64, "N75")
+    cp(T.Lf0[:], T.tri[:], 256, "tri", "Lf00 Lf01")
+    tag[0] = "cw"
+    ts(T.cj[:, 0:8], T.ci[:, 32:40], 15, A.bitwise_and, 64, "ci2", "cj")
+    cp(T.cf[:, 0:40], T.ci[:, 0:40], 64, "ci0 ci1 ci2", "cf")
+    cp(T.cw[:, 0:32], T.ci[:, 0:32], 64, "ci0 ci1", "cw")
+    cp(T.cf[:, 40:48], T.cj[:, 0:8], 64, "cj", "rcol")
+    ts(T.RST[:], T.RR[:, 0:128], 0.0, A.is_equal, 64, "RR", "RST", B24, A.mult)
+    ts(T.thn[0:1, :], T.thi[0:1, :], -16.0, A.mult, 128, "thi", "thn", -16.0, A.add)
+    for j, c in ((0, -8192.0), (1, 0.5), (2, B23 - 15.5), (3, -4607.5), (4, 8192.0)): ms(T.BC[:, j:j + 1], c, 64, "BC%d" % j)
+    ts(T.BC[:, 5:6], rcol, float(TRASH), A.add, 64, "rcol", "BC5")
+    ts(T.BC[:, 6:7], rcol, float(S), A.add, 64, "rcol", "BC6")
+    ts(T.TRI[:], T.RR[:, 0:128], rcol, A.is_gt, 64, "RR rcol", "TRI", -8192.0, A.mult)
+    ts(T.RM[:], T.RR[:], 0.0, A.not_equal, 128, "RR", "RM")
+    ts(T.DM[:], T.RR[:], rcol, A.is_equal, 128, "RR rcol", "DM")
+    act(T.RA[:], T.DM[:, 0:128], F.Copy, 128, "DM", "RA", scale=-B24)
+    ts(T.RT[:], T.DM[:, 0:128], 8192.0, A.mult, 64, "DM", "RT", 1.0, A.max)
+    tt(T.RB[:], T.RT[:], T.RM[:, 0:128], A.mult, 256, "RT RM", "RB")
+    ts(T.JW[:], T.cf[:, 0:16], rcol, A.add, 64, "cf rcol", "JW", -15.0, A.add)
+    tag[0] = "ct"
+    ts(T.tg[:, 0:8], T.cf[:, 17:25], rcol, A.add, 64, "cf rcol", "tg0", 16.0, A.is_lt)
+    tt(T.tg[:, 8:16], T.tg[:, 0:8], T.cf[:, 17:25], A.mult, 64, "tg0 cf", "tg1")
+    tt(T.tg[:, 16:24], T.tg[:, 8:16], T.cf[:, 32:40], A.add, 64, "tg1 cf", "tg2")
+    iota(T.CT[:], [[2304, 2], [0, 128]], -6912, 0, 256, "CT")
+    tag[0] = "cc"
+    for d in range(8): act(T.CR[:, 128 * d:128 * d + 128], T.JR[:, 0:128], F.Abs, 128, "JR tg2", "CR%d" % d, scale=-1.0, col=T.tg[:, 16 + d:17 + d])
+    for d in (0, 4):
+        k = " ".join("CR%d" % j for j in range(d, d + 4)); c = T.CR[:, 128 * d:128 * d + 512]
+        act(c, c, F.Relu, 512, k, k, bias=4, scale=-8192.0)
+
+    def xcols(buf, h, k, step=16): return buf[:, 2048 * h + k:2048 * (h + 1):step]
+    def parts(name, h): return " ".join("%s%d_%d" % (name, h, j) for j in range(NQ))
+
+    def big(out, name, win, wk, off, ok, h):
+        tag[0] = "%s%s%d" % (name, ok, h); q = CFG["q"]
+        for j in range(NQ):
+            c = 128 * h + q * j
+            def f(Q, e, o=out[:, 16 * c:16 * (c + q)], src=off[:, c:c + q]):
+                return Q.tensor_copy(o, win.indirect(src)) if e == "v" else Q.activation(o, win.indirect(src), F.Copy)
+            op(CFG["pat"][len([1 for o in ops if o["lat"] < 0])], f, FX + 16 * q * GA, "%s %s%d" % (wk, ok, h), "%s%d_%d" % (name, h, j), lat=-0.001)
+
+    def energy(h, second):
+        kk = "K%d.k" % h; c = 8 * second
+        for k in range(16): mm(Kb[h][:, k:128:16], xcols(T.X, h, k), T.W8b[:, c:c + 8], False, False, 64, parts("X", h) + " W8b%d" % second, kk)
+        for k in range(8):
+            m = 2048 * h + 256 * k
+            tt(T.M[:, m:m + 256], xcols(T.X, h, k, 8), Yb[h][:, 0:256], A.max, 256, parts("X", h) + " Y%d.y0 Y%d.y1" % (h, h), "M%d_%d" % (h, k))
+            for j in range(2):
+                mm(Kb[h][:, k + 8 * j:128:16], T.M[:, m + j:m + 256:2], T.W8f[:, c:c + 8], False, k + j == 8, 256, "M%d_%d W8f%d" % (h, k, second), kk)
+
+    def front(t, h):
+        y, yk, kk, L, Lk = Yb[h][:, 256:384], "Y%d.s" % h, "K%d.k" % h, T["Lf%d" % t][:, H[h]], "Lf%d%d" % (t, h)
+        key, P = Kb[h][:, 0:128], Pb[h]
+        tag[0] = "ys%d" % h
+        mm(y, I("s16"), T.N75[:], True, False, 128, "Is16 N75", yk)
+        for k in range(16): mm(y, I("s16"), xcols(T.X, h, k), False, k == 15, 128, parts("X", h), yk)
+        for j in range(2): ts(Yb[h][:, j:256:2], y, MAGIC, A.add, 128, yk, "Y%d.y%d" % (h, j), MAGIC, A.subtract)
+        mm(key, I("one"), T.RR[:, 0:128], True, False, 128, "Ione RR", kk)
+        mm(P[:, 0:128], T.IF[:], L, True, False, 512, "IF " + Lk, "P%d.a" % h)
+        tag[0] = "M%d" % h
+        energy(h, 0)
+        tag[0] = "co%d" % h
+        act(T.ysb[:, H[h]], Yb[h][:, 0:256:2], F.Copy, 128, "Y%d.y0" % h, "ysb%d" % h)
+        act(T.KB[:, H[h]], key, F.Copy, 128, kk, "KB%d" % h)
+        scan(T.SM[:, H[h]], T.RST[:], T.KB[:, H[h]], A.add, A.min, 128, "RST KB%d" % h, "SM%d" % h)
+        tt(T.GE[:, H[h]], T.SM[:, H[h]].indirect(T.cw[:, 0:8]), T.KB[:, H[h]], A.is_equal, 128 * GA, "SM%d KB%d cw" % (h, h), "GE%d" % h)
+        mm(P[:, 0:128], T.GE[:, H[h]], I("p8192"), False, True, 128, "GE%d Ip8192" % h, "P%d.a" % h)
+        act(T.tc[:, H[h]], P[:, 0:128], F.Relu, 128, "P%d.a" % h, "tc%d" % h, bias=0)
+        mm(P[:, 128:256], I("one"), T.TRI[:], True, False, 128, "Ione TRI", "P%d.b" % h)
+        mm(P[:, 128:256], T.BO[:], T.tc[:, H[h]], False, True, 512, "BO tc%d" % h, "P%d.b" % h)
+        tag[0] = "dd%d" % h
+        c8, pw = slice(8 * h, 8 * h + 8), T.PW[:, 128 * h + 15:128 * h + 128:16]
+        scan(T.PW[:, H[h]], T.RA[:], P[:, 128:256], A.add, A.max, 128, "RA P%d.b" % h, "PW%d" % h)
+        act(T.QS[:, H[h]], P[:, 128:256], F.Copy, 128, "P%d.b" % h, "QS%d" % h)
+        cp(T.pu[:, c8], pw, 64, "PW%d" % h, "pu%d" % h)
+        tt(T.EP[:, H[h]], T.PW[:, H[h]].indirect(T.cw[:, 0:8]), T.QS[:, H[h]], A.is_equal, 128 * GA, "PW%d cw QS%d" % (h, h), "EP%d" % h)
+        scan(T.SB[:, H[h]], T.RB[:], T.EP[:, H[h]], A.mult, A.add, 64, "RB EP%d" % h, "SB%d" % h)
+        tt(T.pd[:, c8], pw, T.SB[:, 128 * h + 15:128 * h + 128:16], A.add, 64, "PW%d SB%d" % (h, h), "pd%d" % h)
+        ts(T.OFF[:, 16 * h:16 * h + 16:2], T.pd[:, c8], -1.0, A.add, 64, "pd%d BC5" % h, "OFFp%d" % h, T.BC[:, 5:6], A.min)
+        tag[0] = "un%d" % h
+        G = Yb[h][:, 384:512]
+        mm(G, T.ONE[0:1, :], T.thn[0:1, :], True, False, 512, "ONE thn", "Y%d.g" % h)
+        mm(G, T.ysb[:, H[h]], T.WY[:], False, False, 512, "ysb%d WY" % h, "Y%d.g" % h)
+        mm(G, T.IF[:], T.KB[:, H[h]], False, True, 512, "IF KB%d" % h, "Y%d.g" % h)
+        act(T.U[:, H[h]], G, F.Sign, 128, "Y%d.g" % h, "U%d" % h, bias=1)
+        mm(y, T.IF[:], L, True, False, 512, "IF " + Lk, yk)
+        mm(y, T.U[:, H[h]], I("p4608"), False, True, 128, "U%d Ip4608" % h, yk)
+        act(T.VAL[:, c8, 16:32], y, F.Relu, 128, yk, "VALp%d" % h)
+
+    def hosts(t):
+        tag[0] = "vc"
+        for h in (1, 0):
+            for k in range(16): mm(T.VC[:, 8 * h:8 * h + 8, k], xcols(T.V, h, k), T.W8b[:, 24:32], True, True, 64, parts("V", h) + " W8b3", "VC.v")
+        act(T.VS[:, :, 0:16], T.VC[:, 0:16, :], F.Copy, 256, "VC.v", "VSa")
+        act(T.VS[:, :, 16:24], T.VC[:, 0:16, 0:8], F.Copy, 128, "VC.v", "VSb")
+        mm(T.K2[:, 0:16, :], I("one"), T.KC2[:], True, False, 256, "Ione KC2", "K2.k")
+        mm(T.K2[:, 0:16, :], I("one"), T.VS[:, :, 0:16], False, False, 256, "VSa", "K2.k")
+        tag[0] = "eq"
+        for d in range(1, 9):
+            n = 16 if d < 8 else 8; rows = slice(16 * d - 16, 16 * d)
+            tt(T.EQ[:, rows, 0:n], T.VC[:, 0:16, 0:n], T.VS[:, :, d:d + n], A.is_equal, 16 * n, "VC.v VSa VSb", "EQ%d" % d)
+            mm(T.K2[:, 0:16, 0:16 - d], I("p4096"), T.EQ[:, rows, 0:16 - d], False, d == 8, 256 - 16 * d, "Ip4096 EQ%d" % d, "K2.k")
+            if d < 8: mm(T.K2[:, 0:16, 0:d], I("p4096"), T.EQ[:, rows, 16 - d:16], False, False, max(64, 16 * d), "EQ%d" % d, "K2.k")
+        tag[0] = "ho"
+        act(T.KS[:], T.K2[:, 0:16, :], F.Copy, 256, "K2.k", "KS")
+        scan(T.SM2[:], T.RM[:], T.KS[:], A.mult, A.max, 256, "RM KS", "SM2")
+        cp(T.HI[:], T.SM2[:, 15:256:16], 64, "SM2", "HI")
+        ts(T.HJ[:], T.HI[:], 255, A.bitwise_and, 64, "HI", "HJ")
+        tt(T.HD[:], T.HJ[:, 0:16].indirect(T.cw[:, 16:32]), T.DM[:], A.mult, 256 * GA, "HJ cw DM", "HD")
+        for h in range(2): mm(T.K2[:, 17, 8 * h:8 * h + 8], T.HD[:, H[h]], T.W8b[:, 16:24], True, True, 64, "HD W8b2", "K2.h")
+        mm(T.K2[:, 16, :], I("neg"), T.JW[:], True, False, 64, "Ineg JW", "K2.d")
+        for h in range(2): mm(T.K2[:, 16, 8 * h:8 * h + 8], T.HD[:, H[h]], T.W8b[:, 16:24], False, h == 1, 64, "HD", "K2.d")
+        ts(T.e5[:], T.K2[:, 16, :], 0.0, A.is_equal, 64, "K2.d", "e5", -256.0, A.mult)
+        tt(T.HW[:], T.K2[:, 17, :], T.e5[:], A.add, 64, "K2.h e5", "HW")
+        for d in range(8): mm(T.K2[:, 20 + d, :], T.ROT[:, 128 * d:128 * d + 128], T.HW[:], True, True, 64, "ROT HW", "K2.r")
+        ts(T.EH[:], T.K2[:, 20:28, :], 0.0, A.is_equal, 128, "K2.r", "EH")
+        mm(T.K2[:, 18, :], I("one"), T.HW[:], True, False, 64, "Ione HW", "K2.o")
+        mm(T.K2[:, 18, :], I("n32"), T.e5[:], False, False, 64, "In32 e5", "K2.o")
+        for d in range(8): mm(T.K2[:, 18, :], T.CR[:, 128 * d:128 * d + 128], T.EH[:, d, :], False, d == 7, 64, "CR%d EH" % d, "K2.o")
+        ts(T.OFF[:, 1:32:2], T.K2[:, 18, :], T.BC[:, 6:7], A.min, 64, "K2.o BC6", "OFFh", float(DON0 + (S + 16) * t), A.add)
+
+    def back(t, h):
+        b, L, Lk, kk, nw = "P%d.p" % h, T["Lf%d" % t][:, H[h]], "Lf%d%d" % (t, h), "K%d.k" % h, T["nw%d" % t][:, H[h]]
+        p1, p2, key = Pb[h][:, 256:384], Pb[h][:, 384:512], Kb[h][:, 0:128]
+        tag[0] = "pr%d" % h
+        mm(key, T.IF[:], T.KB[:, H[h]], True, False, 512, "IF KB%d" % h, kk)
+        mm(key, T.NA[:, H[h]], I("nB"), False, False, 128, "NA%d InB" % h, kk)
+        mm(Pb[h][:, 256:512], I("one"), T.CT[:], True, False, 256, "Ione CT", b)
+        mm(p2, T.IF[:], L, False, False, 512, "IF " + Lk, b)
+        mm(p1, T.IF[:], T.CP[:, H[h]], False, False, 512, "IF CP%d" % h, b)
+        mm(p1, I("n2304"), T.vs[:, H[h]], False, False, 128, "In2304 vs%d" % h, b)
+        tag[0] = "N%d" % h
+        energy(h, 1)
+        tag[0] = "fi%d" % h
+        act(T.TK[:, H[h]], key, F.Sign, 128, kk, "TK%d" % h, bias=2)
+        mm(p2, T.TK[:, H[h]], I("n4608"), False, False, 128, "TK%d In4608" % h, b)
+        mm(p1, T.TK[:, H[h]], I("p4608"), False, True, 128, "TK%d Ip4608" % h, b)
+        act(T.t2[:, H[h]], p2, F.Relu, 128, b, "t2%d" % h)
+        tt(nw, p1, T.t2[:, H[h]], A.max, 128, b + " t2%d" % h, "nw%d%d" % (t, h))
+        if t == ST - 1:
+            dma("s", "d_y%d" % h, T.yl[:, H[h]], nw, 65536, "nw%d%d" % (t, h), "")
+        else:
+            rid, pid = topo.addr(nxt)[0:2]
+            land = T["Lf%d" % (t + 1)][:, H[h]]; rs = "r%d%d" % (t + 1, h)
+            op("g", lambda q, e: q.remote_dma(land, nw, T.sem[rs], T.sem.sent, pid, rid, topo.mask(core, nxt)), 300.0,
+               "nw%d%d" % (t, h), "", "r", rs, len(topo.engines(core, nxt)), CFG["link"])
+
+    lab, xa, xab = T.win[:, 0:W], T.xw[:, 0:W], T.xw[:, 0:2 * W]
+    for t in range(ST):
+        for h in (1, 0):
+            tag[0] = "lu%d" % h
+            if t:
+                op("x", None, 0.0, "", "Lf%d%d" % (t, h), "x", "r%d%d" % (t, h), len(topo.engines(prv, core)))
+                cp(T.Lu[:, H[h]], T["Lf%d" % t][:, H[h]], 128, "Lf%d%d" % (t, h), "Lu%d" % h)
+            big(T.V, "V", lab, "lab", T.Lu, "Lu", h)
+            big(T.X, "X", xa, "xa", T.Lu, "Lu", h)
+        hosts(t)
+        for h in (1, 0):
+            front(t, h)
+            tag[0] = "sc%d" % h
+            for b in range(8 * h + 7, 8 * h - 1, -1):
+                cp(T.win[:, 0:WN].indirect(T.OFF[:, 2 * b:2 * b + 2]), T.VAL[:, b, :], 32 * CFG["scat"], "OFFp%d OFFh VALj VALp%d" % (h, h), "lab don")
+        if t == ST - 1: dma("s", "d_yb", T.yb[:], T.win[0:128:16, 0:W], 32 * W, "lab", "")
+        for h in (1, 0):
+            tag[0] = "mi%d" % h; pu, d0 = T.pu[:, 8 * h:8 * h + 8], DON0 + (S + 16) * t + 128 * h
+            tt(T.NA[:, H[h]], lab.indirect(pu), T.JR[:, H[h]], A.is_equal, 128 * GA, "lab JR pu%d" % h, "NA%d" % h)
+            tt(T.CD[:, H[h]], T.win[:, d0:d0 + 128], T.NA[:, H[h]], A.mult, 256, "don NA%d" % h, "CD%d" % h)
+            tt(T.CP[:, H[h]], T.nbw[:, 0:W].indirect(pu), T.CD[:, H[h]], A.max, 128 * GA, "nbw pu%d CD%d" % (h, h), "CP%d" % h)
+            cp(T.cu[:, H[h]], T.CP[:, H[h]], 128, "CP%d" % h, "cu%d" % h)
+            act(T.vs[:, H[h]], T.CP[:, H[h]], F.Sign, 128, "CP%d" % h, "vs%d" % h, bias=3)
+        for h in (1, 0): big(T.X, "X", xab, "xa xb", T.cu, "cu", h)
+        for h in (1, 0): back(t, h)
+    if "o" not in ORDER: ORDER["o"] = arrange(ops)[1]
+    emit(g, T, [ops[i] for i in ORDER["o"]])

@@ -1,3 +1,4 @@
+import math
 from concourse.mybir import AluOpType, ActivationFunctionType
 
 W, S, ST, HOP = 4608, 256, 3, 1
@@ -6,93 +7,202 @@ DON0 = W + 16
 WN = DON0 + ST * (S + 16)
 MAGIC = 12582912.0
 B23, B24 = 8388608.0, 16777216.0
+GS = 16384.0
+LS = 1024.0
 ISC = {"one": 1.0, "s16": 0.0625, "p8192": 8192.0, "p4608": 4608.0, "n4608": -4608.0, "n2304": -2304.0,
-       "p4096": 4096.0, "neg": -1.0, "nB": -B23, "n32": -32.0}
+       "p4096": 4096.0, "neg": -1.0, "nB": -B23, "n32": -32.0, "n8192": -8192.0}
 ISN = list(ISC)
 SCRATCH = {}
 for _dt, _list in (
     ("float32", "win:%d lbf:288 thn:128 Lf0:256 Lf1:256 Lf2:256 nw0:256 nw1:256 nw2:256 M:4096 ysb:256 SM:256 tc:256 PW:256 "
-                "QS:256 KB:256 KS:256 SM2:256 pd:16 CD:256 CP:256 t2:256 VAL:16x32 ONE:128 IF:128 BO:128 BT:128 WY:128 B8:16 W8f:24 "
-                "JR:256 BC:16 cf:48 tg:24" % WN),
-    ("bfloat16", "xw:%d X:4096 V:4096 GE:256 EP:256 SB:256 EH:8x16 U:256 NA:256 vs:256 TK:256 VS:16x24 EQ:128x16 HD:256 e5:16 HW:16 "
-                 "IS:%d W8b:32 RR:256 DM:256 TRI:128 RST:128 RA:128 RB:128 RT:128 RM:256 KC2:16x16 N75:128 CT:256 JW:16 ROT:1024 CR:1024"
-                 % (2 * W, 128 * len(ISC))),
+                "QS:256 KB:256 KS:256 SM2:256 pd:16 ROF:1024 CF:8x32 Q1:256 L4:256 IG:128 CP:256 t2:256 VAL:16x32 ONE:128 IF:128 BO:128 BT:128 WY:128 B8:16 W8f:24 "
+                "JR:256 JM:256 BC:16 cf:48 tg:24 lbo:288" % WN),
+    ("bfloat16", "xw:%d X:4096 V:4096 GE:256 EP:256 SB:256 EH:8x16 U:256 R:256 vs:256 TK:256 VS:16x24 EQ:128x16 HD:256 e5:16 HW:16 "
+                 "IS:%d W8b:32 RR:256 DM:256 TRI:128 RST:128 RA:128 RB:128 RT:128 RM:256 KC2:16x16 N75:128 CT:256 JW:16 CI:8x32 ROT:1024 CR:1024 "
+                 "MG:256 O2:256 lbh:288" % (2 * W, 128 * len(ISC))),
     ("int32", "nbw:%d lbs:288 tri:256 thi:128 HI:16 HJ:16 ci:48 cj:8" % W),
-    ("uint16", "Lu:256 cu:256 pu:16 OFF:32 cw:48"),
+    ("uint16", "Lu0:256 Lu1:256 Lu2:256 nu0:256 nu1:256 cu:256 pu:16 OFF:64 cw:48"),
 ):
     for _e in _list.split():
         SCRATCH[_e.split(":")[0]] = ("sbuf", [128] + [int(_x) for _x in _e.split(":")[1].split("x")], _dt)
-BANKS = ("Y0", "Y1", "K0", "K1", "P0", "P1", "VC", "K2")
-for _b in BANKS: SCRATCH[_b] = ("psum", [128, 32, 16] if _b in ("VC", "K2") else [128, 512], "float32")
-SEMAPHORES = (["cv", "ca", "cp", "cg", "sent", "d_lb", "d_tr", "d_th", "d_xa", "d_xb", "d_nb", "d_lab", "d_yb", "d_y0", "d_y1"]
-              + ["r%d%d" % (t, h) for t in range(1, ST) for h in range(2)])
+BANKS = {"Y0": [128, 4], "Y1": [128, 4], "K0": [512], "K1": [512], "P0": [512], "P1": [512], "VC": [32, 16], "K2": [32, 16]}
+for _b in BANKS: SCRATCH[_b] = ("psum", [128] + BANKS[_b], "float32")
+SEMAPHORES = (["cv", "ca", "cp", "cg", "sent", "d_lb", "d_tr", "d_th", "d_xa", "d_xb", "d_nb", "d_lab", "d_yb", "d_yc", "d_y0", "d_y1"]
+              + ["%s%d%d" % (k, t, h) for k in ("Lu", "Lf") for t in range(1, ST) for h in range(2)])
 A, F = AluOpType, ActivationFunctionType
-CFG = {"q": 64, "z": 1152, "gath": 1.55, "scat": 3.5, "fix": 55.0, "pe": 0.5, "link": 3600.0, "slack": [50.0],
-       "pat": "aavavavavaaa" "vavavaaavaaa" "vaavvaaavaaa",
-       "bo": {"cg": 90, "cw": 15, "fi1": 45, "N1": -60, "N0": 10, "XLu1": 15, "pr1": -5, "ys1": 5, "lu1": -15, "vc": -5, "dd0": 15,
-              "ys0": 30, "un1": -5, "mi1": 10, "un0": -30, "c": 90, "Xcu0": 20, "XLu0": 30, "sc0": -5, "mi0": -15, "lu0": 20,
-              "cr": -15, "cv": -60, "co0": 20, "ct": -5, "cc": 20, "sc1": 30, "eq": 90, "ho": 5, "VLu1": -5, "fi0": 20,
-              "VLu0": -5, "dd1": -60}}
+CFG = {"q": 64, "z": 1152, "gath": 1.55, "scat": 3.5, "fix": 55.0, "ind": 55.0, "pe": 0.47, "pf": 3.0, "cyc": 0.93, "dma": 2400.0, "care": 1000.0, "link": 3600.0, "wake": 45.0, "own": 180.0, "late": 80.0, "lump": 600.0, "seed": 1, "tries": 65000, "heat": 300.0, "flip": 1e9, "rep": 2, "lane": 1, "u16": 0, "seedk": True, "join": False, "gift": "vv", "hs": [(1, 0)], "dd": "vv"}
+PLAN = 2 * ["lu1 X1a:a X1b:v y1a y1b V1a:a V1b:v yc1:a yd1:v lu0 M1a M1b V0a:a xs1 M1c M1d vc1 V0b:a vc0 kb1 vs X0a:a eqa eqb ys1:a X0b:a y0a y0b "
+            "yc0:a yd0:a ho co1 hd xs0 M0a M0b un1 M0c M0d ys0:a kb0 un0 sc1 sc0 mi1 co0 C1a:a C1b:a mi0 dd1 dd0 sl0 C0a:a pr1 vv1 "
+            "N1a N1b N1c N1d rs1 C0b:a fi1 vv0 pr0 rs0 N0a N0b N0c N0d fi0"]
 ORDER = {}
 
 
-def banks_of(o): return set(x.split(".")[0] for x in o["r"] + o["w"] if x.split(".")[0] in BANKS)
-
-
-def follow(ops, tensor_in_order):
-    pre = [set() for _ in ops]; lastw, readers, bank = {}, {}, {}
+def follow(ops):
+    pre = [set() for _ in ops]; lastw, readers = {}, {}
     for i, o in enumerate(ops):
         for k in o["r"] + o["w"]:
             if k in lastw: pre[i].add(lastw[k])
         for k in o["w"]: pre[i].update(readers.get(k, []))
-        for k in banks_of(o):
-            for e2, j in bank.setdefault(k, {}).items():
-                if e2 != o["e"] or e2 == "p": pre[i].add(j)
-            bank[k][o["e"]] = i
-        if tensor_in_order and o["e"] == "p": pre[i] = set(j for j in pre[i] if ops[j]["e"] != "p")
         for k in o["r"]: readers.setdefault(k, []).append(i)
         for k in o["w"]:
             lastw[k] = i; readers[k] = []
     return pre
 
 
+def lump(ops):
+    made = set(k for o in ops if o["t"] for k in o["w"]); out = []
+    for o in ops:
+        p = out[-1] if out else None
+        if p and o["e"] == p["e"] == "p" and o["w"] == p["w"] and made & set(o["r"]) <= set(p["r"]) and p["c"] + o["c"] <= CFG["lump"]:
+            out[-1] = dict(p, f=lambda q, e, a=p["f"], b=o["f"]: (a(q, e), b(q, e))[1], c=p["c"] + o["c"], r=p["r"] + o["r"], st=p["st"] or o["st"], sp=o["sp"])
+        else: out.append(o)
+    return out
+
+
 def graph(ops):
-    pre = follow(ops, False); sent, soft = {}, set()
+    pre = follow(ops); sent, soft, closed = {}, set(), {}
     for i, o in enumerate(ops):
         if o["e"] == "s":
-            if "s" in sent: pre[i].add(sent["s"]); soft.add((sent["s"], i))
+            if "s" in sent and sent["s"] not in pre[i]: pre[i].add(sent["s"]); soft.add((sent["s"], i))
             sent["s"] = i
-        if o["k"] == "r": sent[o["sem"]] = i
+        if o["k"] == "r":
+            sent[o["sem"]] = i; soft.update((j, i) for j in pre[i] if ops[j]["k"] == "r")
         if o["k"] == "x": pre[i].add(sent[o["sem"]])
-    suc = [[] for _ in ops]
-    for i in range(len(ops)):
-        for j in pre[i]: suc[j].append(i)
-    return pre, suc, soft
+        if o["e"] == "p":
+            b = o["w"][0].split(".")[0]
+            if o["st"] and b in closed: pre[i].add(closed[b])
+            if o["sp"]: closed[b] = i
+    return pre, soft
 
 
-def arrange(ops, gr=None):
-    pre, suc, soft = gr or graph(ops); n = len(ops); slack = CFG["slack"][0]
-    lv = [0.0] * n
-    for i in range(n - 1, -1, -1): lv[i] = ops[i]["c"] + ops[i]["lat"] + 60.0 + max([lv[j] for j in suc[i]] + [0.0])
-    lv = [v + 100.0 * CFG["bo"].get(o["t"], 0) for v, o in zip(lv, ops)]
-    free = {e: 0.0 for e in "vapgsx"}; at = [0.0] * n; left = [len(p) for p in pre]
-    ready = [i for i in range(n) if not left[i]]; order = []; end = 0.0; dma = 0.0
-    while ready:
-        t0, e = min((max(at[i], free[ops[i]["e"]]), ops[i]["e"]) for i in ready)
-        i = max((i for i in ready if e == ops[i]["e"] and at[i] <= t0 + slack), key=lambda i: lv[i])
-        o = ops[i]; free[e] = max(at[i], free[e]) + o["c"]; done = free[e] + o["lat"]
+def place(ops, order, pre, soft, eng):
+    n = len(ops); wake = CFG["wake"]; t0, t1, done = [0.0] * n, [0.0] * n, [0.0] * n; busy = {}; dma = 0.0
+
+    def clash(k, a, b, e):
+        l = busy.setdefault(k, []); lo, hi = 0, len(l)
+        while lo < hi:
+            m = (lo + hi) // 2
+            if l[m][0] < b: lo = m + 1
+            else: hi = m
+        while lo and l[lo - 1][1] > a + 1e-3:
+            lo -= 1
+            if l[lo][2] != e: return l[lo][1]
+        return None
+    for i in order:
+        o = ops[i]; e = eng[i]; c = o["c"] + (10.0 if e == "a" else 0.0); x = 0.0
+        t = max([t1[j] if (j, i) in soft or eng[j] == e == "p" else done[j] + wake for j in pre[i]] + [0.0])
+        while x is not None:
+            x = clash(e, t, t + c, "")
+            if x is not None: t = x
+            for b in o["b"] if x is None else []:
+                x = clash(b, t - wake, t + c + wake, e)
+                if x is not None:
+                    t = x + wake; break
+        t0[i], t1[i], done[i] = t, t + c, t + c + o["lat"]
+        for k in [e] + o["b"]:
+            busy[k].append((t, t + c, e)); busy[k].sort()
         if o["k"] == "d":
-            dma = max(dma, free[e] + 1200.0) + o["lat"]; done = dma + 800.0
-        order.append(i); ready.remove(i); end = max(end, done)
-        for j in suc[i]:
-            at[j] = max(at[j], free[e] if (i, j) in soft else done + (0.0 if e == "p" and ops[j]["e"] == "p" else 60.0)); left[j] -= 1
-            if not left[j]: ready.append(j)
-    return end, order
+            dma = max(dma, t1[i] + 1200.0) + o["lat"]; done[i] = dma + 800.0
+    return t0, max(done)
+
+
+def arrange(ops):
+    pre, soft = graph(ops); n = len(ops); key = [1e9] * n; eng = [o["e"] for o in ops]
+    for i, o in enumerate(ops):
+        if o["t"]:
+            names = PLAN[min(o["t"][0], 1)].split(); j = [x.split(":")[0] for x in names].index(o["t"][1])
+            key[i] = 1000.0 * o["t"][0] + j
+            if o["e"] == "va": eng[i] = names[j][-1]
+    for i in range(n - 1, -1, -1):
+        for j in pre[i]:
+            if not ops[j]["t"]: key[j] = min(key[j], key[i])
+    key = [k if o["t"] else k * 1e-9 - 2.0 for k, o in zip(key, ops)]
+    for i in range(n): key[i] = max([key[i]] + [key[j] for j in pre[i]])
+    t0, end = place(ops, sorted(range(n), key=lambda i: (key[i], i)), pre, soft, eng)
+    return end, [(i, eng[i]) for i in sorted(range(n), key=lambda i: (t0[i], i))]
+
+
+def improve(ops, order):
+    pre, soft = graph(ops); n = len(ops); own = CFG["own"]; state = [CFG["seed"]]
+    seen = {e: CFG["late"] if e == "v" else CFG["wake"] for e in "vapgsx"}
+    seq = [i for i, e in order]; eng = [e for i, e in sorted(order)]; flex = [i for i in range(n) if ops[i]["e"] == "va"]
+    P = [[(j, (j, i) in soft or ops[j]["e"] == ops[i]["e"] == "p") for j in pre[i]] for i in range(n)]
+    C, L, B, D = [o["c"] for o in ops], [o["lat"] for o in ops], [o["b"] for o in ops], [o["k"] == "d" for o in ops]
+
+    def rnd(m):
+        state[0] = (state[0] * 1103515245 + 12345) % 2147483648; return (state[0] >> 8) % m
+
+    above = [0] * n
+    for i in range(n):
+        far = 0
+        for j in pre[i]: far |= above[j]
+        P[i] = [(j, s) for j, s in P[i] if not far >> j & 1]; above[i] = far | sum(1 << j for j in pre[i])
+    others = [{e: [b + x for b in B[i] for x in "vap" if x != e] for e in ops[i]["e"]} for i in range(n)]
+    mine = [{e: [e] + [b + e for b in B[i]] for e in ops[i]["e"]} for i in range(n)]
+
+    def clock(seq, a, was):
+        t1, near, far, why = was[2][:], was[3][:], was[4][:], was[5][:]; marks = was[6][:a // 32 + 1]
+        last, dma, end, top = marks[-1]; last = dict(last)
+        for p in range(a - a % 32, n):
+            if p % 32 == 0 and p > a: marks.append((dict(last), dma, end, top))
+            i = seq[p]; e = eng[i]; w = last.get(e, -1); t = t1[w]
+            for j, s in P[i]:
+                x = t1[j] if s else near[j] if eng[j] == e else far[j]
+                if x > t: t = x; w = j
+            for k in others[i][e]:
+                j = last.get(k, -1)
+                if far[j] > t: t = far[j]; w = j
+            t += C[i] + (10.0 if e == "a" else 0.0); t1[i] = t; why[i] = w
+            for k in mine[i][e]: last[k] = i
+            if D[i] and "labd" in ops[i]["w"]: t += CFG["dma"] + L[i]
+            elif D[i]:
+                dma = max(dma, t + 0.6 * CFG["dma"]) + L[i]; t = dma + 0.4 * CFG["dma"]
+            else: t += L[i]
+            near[i] = t + own; far[i] = t + seen[e]
+            if t > end: end = t; top = i
+        return end, top, t1, near, far, why, marks
+    now = clock(seq, 0, (0, 0, [0.0] * (n + 1), [0.0] * (n + 1), [0.0] * (n + 1), [-1] * n, [({}, 0.0, 0.0, 0)])); best = (now[0], seq, list(eng))
+    for it in range(CFG["tries"]):
+        arcs = []; i = now[1] if rnd(5) else rnd(n); old = None; why = now[5]
+        while why[i] >= 0:
+            if why[i] not in pre[i]: arcs.append((why[i], i))
+            i = why[i]
+        if rnd(16) == 0:
+            m = flex[rnd(len(flex))]; old = list(eng); eng[m] = "v" if eng[m] == "a" else "a"; new = seq; a = seq.index(m)
+        elif not arcs: continue
+        else:
+            j, i = arcs[rnd(len(arcs))]; a, b = seq.index(j), seq.index(i); far = (0, 0, 0, 2, 5, 15)[rnd(6)]
+            if rnd(2):
+                a = max(0, a - far); need = set(pre[i]); mv = [i]
+                for k in reversed(seq[a:b]):
+                    if k in need: need.update(pre[k]); mv.append(k)
+                if j in mv: continue
+                new = seq[:a] + mv[::-1] + [k for k in seq[a:b] if k not in need] + seq[b + 1:]
+            else:
+                b = min(n - 1, b + far); s = {j}; mv = [j]
+                for k in seq[a + 1:b + 1]:
+                    if not s.isdisjoint(pre[k]): s.add(k); mv.append(k)
+                if i in s: continue
+                new = seq[:a] + [k for k in seq[a:b + 1] if k not in s] + mv + seq[b + 1:]
+        r = clock(new, a, now)
+        if r[0] <= now[0] - (CFG["heat"] * (1.0 - it / CFG["tries"]) + 1.0) * math.log((rnd(4096) + 1) / 4097.0):
+            now = r; seq = new
+            if it % 50 == 0:
+                seq = sorted(seq, key=lambda i: r[2][i] - C[i]); now = clock(seq, 0, now)
+            if now[0] < best[0]: best = (now[0], seq, list(eng))
+        elif old: eng[:] = old
+    return best[0], [(i, best[2][i]) for i in best[1]]
 
 
 def emit(g, T, ops):
     Q = {"v": g.vector, "a": g.scalar, "p": g.tensor, "g": g, "s": g.sync}
-    deps = follow(ops, True)
+    deps = follow(ops); bank = {}
+    for i, o in enumerate(ops):
+        for k in o["b"]:
+            deps[i].update(j for e2, j in bank.setdefault(k, {}).items() if e2 != o["e"])
+            bank[k][o["e"]] = i
+        if o["e"] == "p": deps[i] = set(j for j in deps[i] if ops[j]["e"] != "p")
+        if o["k"] == "r": deps[i] = set(j for j in deps[i] if ops[j]["k"] != "r")
     need = set(j for d in deps for j in d)
     tick, n = {}, {}
     for i, o in enumerate(ops):
@@ -129,12 +239,16 @@ def rank_program(g, core, T, topo):
         return
     nr = len(T.cores)
     nxt, prv = T.cores[(rank + HOP) % nr], T.cores[(rank - HOP) % nr]
-    tag = ["c"]; ops = []; FX, GA, PE = CFG["fix"], CFG["gath"], CFG["pe"]
+    tag = [None]; ops = []; FX, GA, PE = CFG["fix"], CFG["gath"], CFG["pe"]
 
-    def op(e, f, c, r, w, k="c", sem=None, n=0, lat=0.0):
-        ops.append({"e": e, "f": f, "c": c, "r": r.split(), "w": w.split(), "k": k, "sem": sem, "n": n, "lat": lat, "t": tag[0]})
+    def step(t, name): tag[0] = (t, name)
+    def type_of(n): return abs(n - round(n)) > 1e-6 or round(n) in (56, 112)
+    def op(e, f, c, r, w, k="c", sem=None, n=0, lat=0.0, st=False, sp=False):
+        if k == "c" and e in ("v", "a", "va"): c = (CFG["ind"] if type_of(c - FX) else FX) + (c - FX) * CFG["cyc"]
+        banks = sorted(set(x.split(".")[0] for x in (r + " " + w).split()) & set(BANKS))
+        ops.append({"e": e, "f": f, "c": c, "r": r.split(), "w": w.split(), "k": k, "sem": sem, "n": n, "lat": lat, "t": tag[0], "st": st, "sp": sp, "b": banks})
     def dma(e, sem, out, in_, nb, r, w): op(e, lambda q, e: q.dma_start(out, in_), 60.0, r, w, "d", sem, 16, nb / 250.0)
-    def mm(out, l, rh, st, sp, n, r, w): op("p", lambda q, e: q.matmul(out, l, rh, st, sp), n * PE + 5, r, w)
+    def mm(out, l, rh, st, sp, n, r, w): op("p", lambda q, e: q.matmul(out, l, rh, st, sp), n * PE + CFG["pf"], r, w, st=st, sp=sp)
     def cp(out, in_, n, r, w): op("v", lambda q, e: q.tensor_copy(out, in_), FX + n, r, w)
     def tt(out, a, b, o, n, r, w): op("v", lambda q, e: q.tensor_tensor(out, a, b, o), FX + n, r, w)
     def ts(out, a, s1, o0, n, r, w, s2=None, o1=None):
@@ -146,12 +260,18 @@ def rank_program(g, core, T, topo):
         if bias is not None: col, r = T.BC[:, bias:bias + 1], r + " BC%d" % bias
         if col is None: op("a", lambda q, e: q.activation(out, in_, fn, scale=scale), FX + n, r, w)
         else: op("a", lambda q, e: q.activation(out, in_, fn, bias=col, scale=scale), FX + n, r, w)
+    def either(out, in_, n, r, w, e="va"):
+        op(e, lambda q, e: q.tensor_copy(out, in_) if e == "v" else q.activation(out, in_, F.Copy), FX + n, r, w)
+    def put(win, off, val, n, r, w):
+        op("v", lambda q, e: q.tensor_scalar(win.indirect(off), val, 1.0, float(W), A.mult, A.add), FX + n * CFG["scat"], r, w, sem="put")
     def iota(out, pat, base, cm, n, w, fl=True):
         if fl: op("g", lambda q, e: q.iota(out, pat, base, cm, allow_small_or_imprecise_dtypes=True), 130.0 + 2 * n, "", w)
         else: op("g", lambda q, e: q.iota(out, pat, base, cm), 130.0 + 2 * n, "", w)
     def sel(out, in_, pat, cmp, fill, base, cm, n, r, w): op("g", lambda q, e: q.affine_select(out, in_, pat, cmp, fill, base, cm), 170.0 + 2 * n, r, w)
     def I(name):
         j = ISN.index(name); return T.IS[:, 128 * j:128 * j + 128]
+    def whole(out, stop, w):
+        for j in range(2): mm(out, I("one"), T.MG[:, 128 * j:128 * j + 128], False, stop and j == 1, 128, "Ione MG", w)
 
     H = [slice(0, 128), slice(128, 256)]
     Yb, Kb, Pb = [T.Y0, T.Y1], [T.K0, T.K1], [T.P0, T.P1]
@@ -160,15 +280,14 @@ def rank_program(g, core, T, topo):
     dma("s", "d_lb", T.lbs[:], T.lb[:], 32 * W, "", "lbs")
     dma("s", "d_tr", T.tri[:], T.tr[:], 131072, "", "tri")
     dma("s", "d_th", T.thi[0:1, :], T.th[:], 512, "", "thi")
-    dma("s", "d_xa", T.xw[:, 0:W], T.xs[:], 256 * W, "", "xa")
+    dma("s", "d_xa", T.xw[:, 0:W], T.xs[:], 288 * W, "", "xa")
     iota(T.ONE[:], [[0, 128]], 1, 0, 128, "ONE")
     ms(T.win[:, 0:Z], 0.0, Z, "z0"); ms(T.win[:, Z:W - 2 * Z], 0.0, W - 3 * Z, "z1")
     for j in (2, 1): act(T.win[:, W - j * Z:W - j * Z + Z], T.win[:, 0:Z], F.Copy, Z, "z0", "z%d" % (j + 1))
     cp(T.lbf[:], T.lbs[:], 288, "lbs", "lbf")
-    dma("s", "d_lab", T.win[0:128:16, 0:W], T.lbf[:], 32 * W, "lbf", "lab z0 z1 z2 z3")
-    dma("s", "d_nb", T.nbw[:], T.nb[:], 512 * W, "lab", "nbw")
-    dma("s", "d_xb", T.xw[:, W:2 * W], T.xs[:], 256 * W, "lab", "xb")
-    tag[0] = "cg"
+    dma("s", "d_lab", T.win[0:128:16, 0:W], T.lbf[:], 32 * W, "lbf", "lab labd z0 z1 z2 z3")
+    dma("s", "d_nb", T.nbw[:], T.nb[:], 512 * W, "labd", "nbw")
+    dma("s", "d_xb", T.xw[:, W:2 * W], T.xs[:], 256 * W, "", "xb")
     sel(T.IF[:], T.ONE[:], [[-1, 128]], A.is_equal, 0.0, 0, 1, 128, "ONE", "IF")
     sel(T.B8[:, 8:16], T.ONE[:, 0:8], [[-16, 8]], A.is_ge, 0.0, 0, 1, 8, "ONE", "B8t")
     sel(T.B8[:, 0:8], T.B8[:, 8:16], [[16, 8]], A.is_ge, 0.0, 15, -1, 8, "B8t", "B8")
@@ -181,32 +300,29 @@ def rank_program(g, core, T, topo):
     iota(T.ci[:, 32:48], [[0, 16]], 0, 1, 16, "ci2", False)
     iota(T.KC2[:], [[0, 16], [-256, 16]], 3840, 0, 256, "KC2")
     iota(T.JR[:], [[1, 256]], 0, 0, 256, "JR")
-    tag[0] = "cr"
-    iota(T.ROT[:], [[0, 1024]], 0, 0, 1024, "ROT")
-    for pat, cmp, fill, base, cm in (([[1, 8], [1, 128]], A.not_equal, 1.0, 1, -1), ([[1, 8], [1, 128]], A.not_equal, 1.0, -15, -1),
-                                     ([[0, 8], [1, 128]], A.not_equal, -1.0, 0, -1), ([[0, 8], [-16, 8], [0, 16]], A.is_ge, 0.0, 0, 1),
-                                     ([[0, 8], [16, 8], [0, 16]], A.is_ge, 0.0, 15, -1)):
-        sel(T.ROT[:], T.ROT[:], pat, cmp, fill, base, cm, 1024, "ROT", "ROT")
-    iota(T.VAL[:], [[16, 16], [1, 32]], 0, 0, 512, "VALp0 VALp1 VALj")
+    iota(T.O2[:], [[0, 256]], 1, 0, 256, "O2")
+    sel(T.CI[:], T.O2[:], [[-16, 8], [0, 2], [-1, 16]], A.is_equal, 0.0, 0, 1, 256, "O2", "CI")
+    for d in range(8): sel(T.ROT[:, 128 * d:128 * d + 128], T.CI[:, :, d + 1:d + 17], [[-1, 128]], A.not_equal, -1.0, 0, 1, 128, "CI", "ROT%d" % d)
+    for d in range(8 if "p" in CFG["dd"] else 0): sel(T.ROF[:, 128 * d:128 * d + 128], T.ROT[:, 128 * d:128 * d + 128], [[0, 128]], A.is_ge, 0.0, 0, 1, 128, "ROT%d" % d, "ROF%d" % d)
+    iota(T.VAL[:], [[16, 16], [0, 2], [1, 16]], -W, 0, 512, "VALp0 VALp1 VALj")
     iota(T.win[:, W:WN], [[0, WN - W]], 0, 0, WN - W, "don")
-    tag[0] = "ca"
     for nm in ISN: act(I(nm), T.IF[:], F.Copy, 128, "IF", "I" + nm, scale=ISC[nm])
     for j, c in enumerate((-16.0, 16.0, 1.0)): act(T.W8b[:, 8 * j:8 * j + 8], T.B8[:, 0:8], F.Copy, 64, "B8", "W8b%d" % j, scale=c)
     act(T.W8b[:, 24:32], T.W8f[:, 16:24], F.Copy, 64, "Wself", "W8b3")
     for j, c in enumerate((32.0, -32.0)): act(T.W8f[:, 8 * j:8 * j + 8], T.B8[:, 0:8], F.Copy, 64, "B8", "W8f%d" % j, scale=c)
-    act(T.WY[:], T.BO[:], F.Copy, 128, "BO", "WY", scale=-16.0)
-    tag[0] = "cv"
-    cp(T.Lu[:], T.tri[:], 256, "tri", "Lu0 Lu1")
+    act(T.WY[:], T.BO[:], F.Copy, 128, "BO", "WY", scale=-16.0 * GS)
+    act(T.IG[:], T.IF[:], F.Copy, 128, "IF", "IG", scale=GS)
+    cp(T.Lu0[:], T.tri[:], 256, "tri", "Lu00 Lu01")
     ms(T.N75[:], -7.5, 64, "N75")
+    ms(T.MG[:, 0:128], MAGIC, 64, "MG"); ms(T.MG[:, 128:256], -MAGIC, 64, "MG")
     cp(T.Lf0[:], T.tri[:], 256, "tri", "Lf00 Lf01")
-    tag[0] = "cw"
     ts(T.cj[:, 0:8], T.ci[:, 32:40], 15, A.bitwise_and, 64, "ci2", "cj")
     cp(T.cf[:, 0:40], T.ci[:, 0:40], 64, "ci0 ci1 ci2", "cf")
     cp(T.cw[:, 0:32], T.ci[:, 0:32], 64, "ci0 ci1", "cw")
     cp(T.cf[:, 40:48], T.cj[:, 0:8], 64, "cj", "rcol")
     ts(T.RST[:], T.RR[:, 0:128], 0.0, A.is_equal, 64, "RR", "RST", B24, A.mult)
-    ts(T.thn[0:1, :], T.thi[0:1, :], -16.0, A.mult, 128, "thi", "thn", -16.0, A.add)
-    for j, c in ((0, -8192.0), (1, 0.5), (2, B23 - 15.5), (3, -4607.5), (4, 8192.0)): ms(T.BC[:, j:j + 1], c, 64, "BC%d" % j)
+    ts(T.thn[0:1, :], T.thi[0:1, :], -16.0 * GS, A.mult, 128, "thi", "thn", -15.0 * GS, A.add)
+    for j, c in ((0, -8192.0), (1, float(W)), (2, -15.5), (3, -4607.5), (4, 8192.0)): ms(T.BC[:, j:j + 1], c, 64, "BC%d" % j)
     ts(T.BC[:, 5:6], rcol, float(TRASH), A.add, 64, "rcol", "BC5")
     ts(T.BC[:, 6:7], rcol, float(S), A.add, 64, "rcol", "BC6")
     ts(T.TRI[:], T.RR[:, 0:128], rcol, A.is_gt, 64, "RR rcol", "TRI", -8192.0, A.mult)
@@ -216,12 +332,10 @@ def rank_program(g, core, T, topo):
     ts(T.RT[:], T.DM[:, 0:128], 8192.0, A.mult, 64, "DM", "RT", 1.0, A.max)
     tt(T.RB[:], T.RT[:], T.RM[:, 0:128], A.mult, 256, "RT RM", "RB")
     ts(T.JW[:], T.cf[:, 0:16], rcol, A.add, 64, "cf rcol", "JW", -15.0, A.add)
-    tag[0] = "ct"
     ts(T.tg[:, 0:8], T.cf[:, 17:25], rcol, A.add, 64, "cf rcol", "tg0", 16.0, A.is_lt)
     tt(T.tg[:, 8:16], T.tg[:, 0:8], T.cf[:, 17:25], A.mult, 64, "tg0 cf", "tg1")
     tt(T.tg[:, 16:24], T.tg[:, 8:16], T.cf[:, 32:40], A.add, 64, "tg1 cf", "tg2")
     iota(T.CT[:], [[2304, 2], [0, 128]], -6912, 0, 256, "CT")
-    tag[0] = "cc"
     for d in range(8): act(T.CR[:, 128 * d:128 * d + 128], T.JR[:, 0:128], F.Abs, 128, "JR tg2", "CR%d" % d, scale=-1.0, col=T.tg[:, 16 + d:17 + d])
     for d in (0, 4):
         k = " ".join("CR%d" % j for j in range(d, d + 4)); c = T.CR[:, 128 * d:128 * d + 512]
@@ -231,143 +345,170 @@ def rank_program(g, core, T, topo):
     def parts(name, h): return " ".join("%s%d_%d" % (name, h, j) for j in range(NQ))
 
     def big(out, name, win, wk, off, ok, h):
-        tag[0] = "%s%s%d" % (name, ok, h); q = CFG["q"]
+        q = CFG["q"]
         for j in range(NQ):
-            c = 128 * h + q * j
-            def f(Q, e, o=out[:, 16 * c:16 * (c + q)], src=off[:, c:c + q]):
-                return Q.tensor_copy(o, win.indirect(src)) if e == "v" else Q.activation(o, win.indirect(src), F.Copy)
-            op(CFG["pat"][len([1 for o in ops if o["lat"] < 0])], f, FX + 16 * q * GA, "%s %s%d" % (wk, ok, h), "%s%d_%d" % (name, h, j), lat=-0.001)
+            c = 128 * h + q * j; step(t, "%s%d%s" % ("C" if ok == "cu" else name, h, "abcd"[j]))
+            either(out[:, 16 * c:16 * (c + q)], win.indirect(off[:, c:c + q]), 16 * q * GA, "%s %s%d" % (wk, ok, h), "%s%d_%d" % (name, h, j))
 
-    def energy(h, second):
+    def energy(t, h, second, stop):
         kk = "K%d.k" % h; c = 8 * second
         for k in range(16): mm(Kb[h][:, k:128:16], xcols(T.X, h, k), T.W8b[:, c:c + 8], False, False, 64, parts("X", h) + " W8b%d" % second, kk)
-        for k in range(8):
-            m = 2048 * h + 256 * k
-            tt(T.M[:, m:m + 256], xcols(T.X, h, k, 8), Yb[h][:, 0:256], A.max, 256, parts("X", h) + " Y%d.y0 Y%d.y1" % (h, h), "M%d_%d" % (h, k))
-            for j in range(2):
-                mm(Kb[h][:, k + 8 * j:128:16], T.M[:, m + j:m + 256:2], T.W8f[:, c:c + 8], False, k + j == 8, 256, "M%d_%d W8f%d" % (h, k, second), kk)
+        R = CFG["rep"]; n = 16 // R
+        for k in range(n):
+            m = 2048 * h + 128 * R * k; step(t, "%s%d%s" % ("MN"[second], h, "abcd"[k * R // 4]))
+            tt(T.M[:, m:m + 128 * R], xcols(T.X, h, k, n), Yb[h][:, :, 0:R], A.max, 128 * R, parts("X", h) + " Y%d.y0 Y%d.y1 Y%d.y2" % (h, h, h), "M%d_%d" % (h, k))
+            for j in range(R):
+                mm(Kb[h][:, k + n * j:128:16], T.M[:, m + j:m + 128 * R:R], T.W8f[:, c:c + 8], False, stop and k + j == n + R - 2, 256, "M%d_%d W8f%d" % (h, k, second), kk)
 
     def front(t, h):
-        y, yk, kk, L, Lk = Yb[h][:, 256:384], "Y%d.s" % h, "K%d.k" % h, T["Lf%d" % t][:, H[h]], "Lf%d%d" % (t, h)
+        y, yk, kk, L, Lk = Yb[h][:, :, 0], "Y%d.y0" % h, "K%d.k" % h, T["Lf%d" % t][:, H[h]], "Lf%d%d" % (t, h)
         key, P = Kb[h][:, 0:128], Pb[h]
-        tag[0] = "ys%d" % h
+        step(t, "y%da" % h)
         mm(y, I("s16"), T.N75[:], True, False, 128, "Is16 N75", yk)
-        for k in range(16): mm(y, I("s16"), xcols(T.X, h, k), False, k == 15, 128, parts("X", h), yk)
-        for j in range(2): ts(Yb[h][:, j:256:2], y, MAGIC, A.add, 128, yk, "Y%d.y%d" % (h, j), MAGIC, A.subtract)
+        for k in range(16):
+            step(t, "y%d%s" % (h, "ab"[k // 8])); mm(y, I("s16"), xcols(T.X, h, k), False, False, 128, parts("X", h), yk)
+        whole(y, True, yk)
+        step(t, "yc%d" % h)
+        if CFG["rep"] > 1: either(Yb[h][:, :, 1], y, 128, yk, "Y%d.y1" % h)
+        step(t, "yd%d" % h)
+        if CFG["rep"] > 2: either(Yb[h][:, :, 2:4], Yb[h][:, :, 0:2], 256, yk + " Y%d.y1" % h, "Y%d.y2" % h)
+        step(t, "ys%d" % h); either(T.ysb[:, H[h]], y, 128, yk, "ysb%d" % h)
+        step(t, "xs%d" % h)
         mm(key, I("one"), T.RR[:, 0:128], True, False, 128, "Ione RR", kk)
         mm(P[:, 0:128], T.IF[:], L, True, False, 512, "IF " + Lk, "P%d.a" % h)
-        tag[0] = "M%d" % h
-        energy(h, 0)
-        tag[0] = "co%d" % h
-        act(T.ysb[:, H[h]], Yb[h][:, 0:256:2], F.Copy, 128, "Y%d.y0" % h, "ysb%d" % h)
+        energy(t, h, 0, CFG["seedk"])
+        step(t, "kb%d" % h)
         act(T.KB[:, H[h]], key, F.Copy, 128, kk, "KB%d" % h)
+        step(t, "co%d" % h)
         scan(T.SM[:, H[h]], T.RST[:], T.KB[:, H[h]], A.add, A.min, 128, "RST KB%d" % h, "SM%d" % h)
         tt(T.GE[:, H[h]], T.SM[:, H[h]].indirect(T.cw[:, 0:8]), T.KB[:, H[h]], A.is_equal, 128 * GA, "SM%d KB%d cw" % (h, h), "GE%d" % h)
         mm(P[:, 0:128], T.GE[:, H[h]], I("p8192"), False, True, 128, "GE%d Ip8192" % h, "P%d.a" % h)
         act(T.tc[:, H[h]], P[:, 0:128], F.Relu, 128, "P%d.a" % h, "tc%d" % h, bias=0)
         mm(P[:, 128:256], I("one"), T.TRI[:], True, False, 128, "Ione TRI", "P%d.b" % h)
         mm(P[:, 128:256], T.BO[:], T.tc[:, H[h]], False, True, 512, "BO tc%d" % h, "P%d.b" % h)
-        tag[0] = "dd%d" % h
         c8, pw = slice(8 * h, 8 * h + 8), T.PW[:, 128 * h + 15:128 * h + 128:16]
         scan(T.PW[:, H[h]], T.RA[:], P[:, 128:256], A.add, A.max, 128, "RA P%d.b" % h, "PW%d" % h)
-        act(T.QS[:, H[h]], P[:, 128:256], F.Copy, 128, "P%d.b" % h, "QS%d" % h)
         cp(T.pu[:, c8], pw, 64, "PW%d" % h, "pu%d" % h)
-        tt(T.EP[:, H[h]], T.PW[:, H[h]].indirect(T.cw[:, 0:8]), T.QS[:, H[h]], A.is_equal, 128 * GA, "PW%d cw QS%d" % (h, h), "EP%d" % h)
-        scan(T.SB[:, H[h]], T.RB[:], T.EP[:, H[h]], A.mult, A.add, 64, "RB EP%d" % h, "SB%d" % h)
-        tt(T.pd[:, c8], pw, T.SB[:, 128 * h + 15:128 * h + 128:16], A.add, 64, "PW%d SB%d" % (h, h), "pd%d" % h)
-        ts(T.OFF[:, 16 * h:16 * h + 16:2], T.pd[:, c8], -1.0, A.add, 64, "pd%d BC5" % h, "OFFp%d" % h, T.BC[:, 5:6], A.min)
-        tag[0] = "un%d" % h
-        G = Yb[h][:, 384:512]
-        mm(G, T.ONE[0:1, :], T.thn[0:1, :], True, False, 512, "ONE thn", "Y%d.g" % h)
-        mm(G, T.ysb[:, H[h]], T.WY[:], False, False, 512, "ysb%d WY" % h, "Y%d.g" % h)
-        mm(G, T.IF[:], T.KB[:, H[h]], False, True, 512, "IF KB%d" % h, "Y%d.g" % h)
-        act(T.U[:, H[h]], G, F.Sign, 128, "Y%d.g" % h, "U%d" % h, bias=1)
-        mm(y, T.IF[:], L, True, False, 512, "IF " + Lk, yk)
-        mm(y, T.U[:, H[h]], I("p4608"), False, True, 128, "U%d Ip4608" % h, yk)
-        act(T.VAL[:, c8, 16:32], y, F.Relu, 128, yk, "VALp%d" % h)
+        step(t, "dd%d" % h)
+        off = T.OFF[:, 17:32:2] if h and CFG["join"] else T.OFF[:, 32 + 16 * h:48 + 16 * h:2]
+        if CFG["dd"][h] == "v":
+            act(T.QS[:, H[h]], P[:, 128:256], F.Copy, 128, "P%d.b" % h, "QS%d" % h)
+            tt(T.EP[:, H[h]], T.PW[:, H[h]].indirect(T.cw[:, 0:8]), T.QS[:, H[h]], A.is_equal, 128 * GA, "PW%d cw QS%d" % (h, h), "EP%d" % h)
+            scan(T.SB[:, H[h]], T.RB[:], T.EP[:, H[h]], A.mult, A.add, 64, "RB EP%d" % h, "SB%d" % h)
+            tt(T.pd[:, c8], pw, T.SB[:, 128 * h + 15:128 * h + 128:16], A.add, 64, "PW%d SB%d" % (h, h), "pd%d" % h)
+            ts(off, T.pd[:, c8], -1.0, A.add, 64, "pd%d BC5" % h, "OFFp%d" % h, T.BC[:, 5:6], A.min)
+        else:
+            for d in range(8): mm(P[:, 8 * d:8 * d + 8], T.ROF[:, 128 * d:128 * d + 128], pw, True, True, 256, "ROF%d PW%d" % (d, h), "P%d.a" % h)
+            ts(T.EP[:, 64 * h:64 * h + 64], P[:, 0:64], 0.0, A.is_equal, 64, "P%d.a" % h, "EP%d" % h)
+            mm(P[:, 64:72], T.IF[:], pw, True, False, 256, "IF PW%d" % h, "P%d.a" % h)
+            for d in range(8): mm(P[:, 64:72], T.CR[:, 128 * d:128 * d + 128], T.EP[:, 64 * h + 8 * d:64 * h + 8 * d + 8], False, d == 7, 64, "CR%d EP%d" % (d, h), "P%d.a" % h)
+            ts(off, P[:, 64:72], T.BC[:, 5:6], A.min, 64, "P%d.a BC5" % h, "OFFp%d" % h)
+        step(t, "un%d" % h)
+        G, D = T.VC[:, 16 + 8 * h:24 + 8 * h, :], Kb[h][:, 256:384]
+        mm(G, T.thn[0:1, :], T.ONE[0:1, :], True, False, 512, "ONE thn", "VC.g%d" % h)
+        mm(G, T.WY[:], T.ysb[:, H[h]], False, False, 512, "ysb%d WY" % h, "VC.g%d" % h)
+        mm(G, T.KB[:, H[h]], T.IG[:], False, CFG["gift"][h] == "a", 512, "IG KB%d" % h, "VC.g%d" % h)
+        if CFG["gift"][h] == "v":
+            mm(G, I("n8192"), T.O2[:, 0:128], False, True, 128, "In8192 O2", "VC.g%d" % h)
+            tt(T.VAL[:, c8, 0:16], G, L, A.min, 128, "VC.g%d %s" % (h, Lk), "VALp%d" % h)
+        else:
+            act(T.U[:, H[h]], G, F.Sign, 128, "VC.g%d" % h, "U%d" % h, bias=0)
+            mm(D, T.IF[:], L, True, False, 512, "IF " + Lk, "K%d.d" % h)
+            mm(D, I("p8192"), T.U[:, H[h]], False, True, 128, "U%d Ip8192" % h, "K%d.d" % h)
+            act(T.VAL[:, c8, 0:16], D, F.Identity, 128, "K%d.d" % h, "VALp%d" % h, bias=0)
 
-    def hosts(t):
-        tag[0] = "vc"
-        for h in (1, 0):
-            for k in range(16): mm(T.VC[:, 8 * h:8 * h + 8, k], xcols(T.V, h, k), T.W8b[:, 24:32], True, True, 64, parts("V", h) + " W8b3", "VC.v")
-        act(T.VS[:, :, 0:16], T.VC[:, 0:16, :], F.Copy, 256, "VC.v", "VSa")
-        act(T.VS[:, :, 16:24], T.VC[:, 0:16, 0:8], F.Copy, 128, "VC.v", "VSb")
-        mm(T.K2[:, 0:16, :], I("one"), T.KC2[:], True, False, 256, "Ione KC2", "K2.k")
-        mm(T.K2[:, 0:16, :], I("one"), T.VS[:, :, 0:16], False, False, 256, "VSa", "K2.k")
-        tag[0] = "eq"
+    def hosts(t, hs):
+        a, b = 8 * min(hs), 8 * max(hs) + 8; r = slice(a, b); c = slice(16 * a, 16 * b); m = b - a; s = "" if m == 16 else str(hs[0])
+        def ks(*names): return " ".join(x + str(h) for x in names for h in hs)
+        step(t, "vs" + s)
+        act(T.VS[:, r, 0:16], T.VC[:, r, :], F.Copy, 16 * m, ks("VC.v"), ks("VSa"))
+        act(T.VS[:, r, 16:24], T.VC[:, r, 0:8], F.Copy, 8 * m, ks("VC.v"), ks("VSb"))
+        mm(T.K2[:, r, :], I("one"), T.KC2[:, r, :], True, False, 16 * m, "Ione KC2", ks("K2.k"))
+        mm(T.K2[:, r, :], I("one"), T.VS[:, r, 0:16], False, False, 16 * m, ks("VSa"), ks("K2.k"))
         for d in range(1, 9):
-            n = 16 if d < 8 else 8; rows = slice(16 * d - 16, 16 * d)
-            tt(T.EQ[:, rows, 0:n], T.VC[:, 0:16, 0:n], T.VS[:, :, d:d + n], A.is_equal, 16 * n, "VC.v VSa VSb", "EQ%d" % d)
-            mm(T.K2[:, 0:16, 0:16 - d], I("p4096"), T.EQ[:, rows, 0:16 - d], False, d == 8, 256 - 16 * d, "Ip4096 EQ%d" % d, "K2.k")
-            if d < 8: mm(T.K2[:, 0:16, 0:d], I("p4096"), T.EQ[:, rows, 16 - d:16], False, False, max(64, 16 * d), "EQ%d" % d, "K2.k")
-        tag[0] = "ho"
-        act(T.KS[:], T.K2[:, 0:16, :], F.Copy, 256, "K2.k", "KS")
-        scan(T.SM2[:], T.RM[:], T.KS[:], A.mult, A.max, 256, "RM KS", "SM2")
-        cp(T.HI[:], T.SM2[:, 15:256:16], 64, "SM2", "HI")
-        ts(T.HJ[:], T.HI[:], 255, A.bitwise_and, 64, "HI", "HJ")
-        tt(T.HD[:], T.HJ[:, 0:16].indirect(T.cw[:, 16:32]), T.DM[:], A.mult, 256 * GA, "HJ cw DM", "HD")
-        for h in range(2): mm(T.K2[:, 17, 8 * h:8 * h + 8], T.HD[:, H[h]], T.W8b[:, 16:24], True, True, 64, "HD W8b2", "K2.h")
-        mm(T.K2[:, 16, :], I("neg"), T.JW[:], True, False, 64, "Ineg JW", "K2.d")
-        for h in range(2): mm(T.K2[:, 16, 8 * h:8 * h + 8], T.HD[:, H[h]], T.W8b[:, 16:24], False, h == 1, 64, "HD", "K2.d")
-        ts(T.e5[:], T.K2[:, 16, :], 0.0, A.is_equal, 64, "K2.d", "e5", -256.0, A.mult)
-        tt(T.HW[:], T.K2[:, 17, :], T.e5[:], A.add, 64, "K2.h e5", "HW")
-        for d in range(8): mm(T.K2[:, 20 + d, :], T.ROT[:, 128 * d:128 * d + 128], T.HW[:], True, True, 64, "ROT HW", "K2.r")
-        ts(T.EH[:], T.K2[:, 20:28, :], 0.0, A.is_equal, 128, "K2.r", "EH")
-        mm(T.K2[:, 18, :], I("one"), T.HW[:], True, False, 64, "Ione HW", "K2.o")
-        mm(T.K2[:, 18, :], I("n32"), T.e5[:], False, False, 64, "In32 e5", "K2.o")
-        for d in range(8): mm(T.K2[:, 18, :], T.CR[:, 128 * d:128 * d + 128], T.EH[:, d, :], False, d == 7, 64, "CR%d EH" % d, "K2.o")
-        ts(T.OFF[:, 1:32:2], T.K2[:, 18, :], T.BC[:, 6:7], A.min, 64, "K2.o BC6", "OFFh", float(DON0 + (S + 16) * t), A.add)
+            n = 16 if d < 8 else 8; rows = slice(16 * d - 16 + a, 16 * d - 16 + b); step(t, "eq" + "ab"[d // 5] + s); eq = ks("EQ%d" % d)
+            tt(T.EQ[:, rows, 0:n], T.VC[:, r, 0:n], T.VS[:, r, d:d + n], A.is_equal, m * n, ks("VC.v", "VSa", "VSb"), eq)
+            mm(T.K2[:, r, 0:16 - d], I("p4096"), T.EQ[:, rows, 0:16 - d], False, d == 8, max(64, m * (16 - d)), "Ip4096 " + eq, ks("K2.k"))
+            if d < 8: mm(T.K2[:, r, 0:d], I("p4096"), T.EQ[:, rows, 16 - d:16], False, False, max(64, m * d), eq, ks("K2.k"))
+        step(t, "ho" + s)
+        act(T.KS[:, c], T.K2[:, r, :], F.Copy, 16 * m, ks("K2.k"), ks("KS"))
+        scan(T.SM2[:, c], T.RM[:, c], T.KS[:, c], A.mult, A.max, 16 * m, "RM " + ks("KS"), ks("SM2"))
+        cp(T.HI[:, r], T.SM2[:, 16 * a + 15:16 * b:16], 64, ks("SM2"), ks("HI"))
+        ts(T.HJ[:, r], T.HI[:, r], 255, A.bitwise_and, 64, ks("HI"), ks("HJ"))
+        tt(T.HD[:, c], T.HJ[:, r].indirect(T.cw[:, 16:16 + m]), T.DM[:, c], A.mult, 16 * m * GA, "cw DM " + ks("HJ"), ks("HD"))
+        for h in hs: mm(T.K2[:, 17, 8 * h:8 * h + 8], T.HD[:, H[h]], T.W8b[:, 16:24], True, True, 64, "W8b2 " + ks("HD"), ks("K2.h"))
+        mm(T.K2[:, 16, r], I("neg"), T.JW[:, r], True, False, 64, "Ineg JW", ks("K2.d"))
+        for h in hs: mm(T.K2[:, 16, 8 * h:8 * h + 8], T.HD[:, H[h]], T.W8b[:, 16:24], False, h == hs[-1], 64, ks("HD"), ks("K2.d"))
+        step(t, "hd" + s)
+        ts(T.e5[:, r], T.K2[:, 16, r], 0.0, A.is_equal, 64, ks("K2.d"), ks("e5"), -256.0, A.mult)
+        tt(T.HW[:, r], T.K2[:, 17, r], T.e5[:, r], A.add, 64, ks("K2.h", "e5"), ks("HW"))
+        for d in range(8):
+            mm(T.K2[:, 20 + d, r], T.ROT[:, 128 * d:128 * d + 128], T.HW[:, r], True, True, 64, "ROT%d " % d + ks("HW"), ks("K2.r"))
+        ts(T.EH[:, :, r], T.K2[:, 20:28, r], 0.0, A.is_equal, 8 * m, ks("K2.r"), ks("EH"))
+        mm(T.K2[:, 18, r], I("one"), T.HW[:, r], True, False, 64, "Ione " + ks("HW"), ks("K2.o"))
+        mm(T.K2[:, 18, r], I("n32"), T.e5[:, r], False, False, 64, "In32 " + ks("e5"), ks("K2.o"))
+        for d in range(8): mm(T.K2[:, 18, r], T.CR[:, 128 * d:128 * d + 128], T.EH[:, d, r], False, d == 7, 64, "CR%d " % d + ks("EH"), ks("K2.o"))
+        ts(T.OFF[:, 2 * a:2 * b:2], T.K2[:, 18, r], T.BC[:, 6:7], A.min, 64, "BC6 " + ks("K2.o"), ks("OFFh"), float(DON0 * CFG["join"] + (S + 16) * t), A.add)
 
     def back(t, h):
         b, L, Lk, kk, nw = "P%d.p" % h, T["Lf%d" % t][:, H[h]], "Lf%d%d" % (t, h), "K%d.k" % h, T["nw%d" % t][:, H[h]]
         p1, p2, key = Pb[h][:, 256:384], Pb[h][:, 384:512], Kb[h][:, 0:128]
-        tag[0] = "pr%d" % h
-        mm(key, T.IF[:], T.KB[:, H[h]], True, False, 512, "IF KB%d" % h, kk)
-        mm(key, T.NA[:, H[h]], I("nB"), False, False, 128, "NA%d InB" % h, kk)
+        step(t, "pr%d" % h)
+        if CFG["seedk"]: mm(key, T.IF[:], T.KB[:, H[h]], True, False, 512, "IF KB%d" % h, kk)
         mm(Pb[h][:, 256:512], I("one"), T.CT[:], True, False, 256, "Ione CT", b)
         mm(p2, T.IF[:], L, False, False, 512, "IF " + Lk, b)
         mm(p1, T.IF[:], T.CP[:, H[h]], False, False, 512, "IF CP%d" % h, b)
         mm(p1, I("n2304"), T.vs[:, H[h]], False, False, 128, "In2304 vs%d" % h, b)
-        tag[0] = "N%d" % h
-        energy(h, 1)
-        tag[0] = "fi%d" % h
+        energy(t, h, 1, False)
+        step(t, "rs%d" % h)
+        tt(T.R[:, H[h]], lab.indirect(T.pu[:, 8 * h:8 * h + 8]), T.JR[:, H[h]], A.is_lt, 128 * GA, "lab JR pu%d" % h, "R%d" % h)
+        tt(T.Q1[:, H[h]], T.nbw[:, 0:W].indirect(T.pu[:, 8 * h:8 * h + 8]), T.R[:, H[h]], A.mult, 128 * GA, "nbw pu%d R%d" % (h, h), "Q1%d" % h)
+        mm(p2, I("n8192"), T.R[:, H[h]], False, False, 128, "In8192 R%d" % h, b)
+        step(t, "fi%d" % h)
+        mm(key, T.R[:, H[h]], I("nB"), False, True, 128, "R%d InB" % h, kk)
         act(T.TK[:, H[h]], key, F.Sign, 128, kk, "TK%d" % h, bias=2)
         mm(p2, T.TK[:, H[h]], I("n4608"), False, False, 128, "TK%d In4608" % h, b)
         mm(p1, T.TK[:, H[h]], I("p4608"), False, True, 128, "TK%d Ip4608" % h, b)
-        act(T.t2[:, H[h]], p2, F.Relu, 128, b, "t2%d" % h)
+        tt(T.t2[:, H[h]], p2, T.Q1[:, H[h]], A.max, 128, b + " Q1%d" % h, "t2%d" % h)
         tt(nw, p1, T.t2[:, H[h]], A.max, 128, b + " t2%d" % h, "nw%d%d" % (t, h))
         if t == ST - 1:
             dma("s", "d_y%d" % h, T.yl[:, H[h]], nw, 65536, "nw%d%d" % (t, h), "")
         else:
             rid, pid = topo.addr(nxt)[0:2]
-            land = T["Lf%d" % (t + 1)][:, H[h]]; rs = "r%d%d" % (t + 1, h)
-            op("g", lambda q, e: q.remote_dma(land, nw, T.sem[rs], T.sem.sent, pid, rid, topo.mask(core, nxt)), 300.0,
-               "nw%d%d" % (t, h), "", "r", rs, len(topo.engines(core, nxt)), CFG["link"])
+            if CFG["u16"]: cp(T["nu%d" % t][:, H[h]], nw, 128, "nw%d%d" % (t, h), "nu%d%d" % (t, h))
+            for src, dst, lat in (("nu", "Lu", CFG["link"] * 0.8), ("nw", "Lf", CFG["link"]))[1 - CFG["u16"]:]:
+                def send(q, e, src=T["%s%d" % (src, t)][:, H[h]], dst=T["%s%d" % (dst, t + 1)][:, H[h]], sem=T.sem["%s%d%d" % (dst, t + 1, h)]):
+                    return q.remote_dma(dst, src, sem, T.sem.sent, pid, rid, sum(1 << m for m in lanes(core, nxt)))
+                op("g", send, 300.0, "%s%d%d" % (src, t, h), "sent", "r", "%s%d%d" % (dst, t + 1, h), len(lanes(core, nxt)), lat)
 
+    def lanes(a, b): return topo.engines(a, b)[::CFG["lane"]]
     lab, xa, xab = T.win[:, 0:W], T.xw[:, 0:W], T.xw[:, 0:2 * W]
     for t in range(ST):
         for h in (1, 0):
-            tag[0] = "lu%d" % h
-            if t:
-                op("x", None, 0.0, "", "Lf%d%d" % (t, h), "x", "r%d%d" % (t, h), len(topo.engines(prv, core)))
-                cp(T.Lu[:, H[h]], T["Lf%d" % t][:, H[h]], 128, "Lf%d%d" % (t, h), "Lu%d" % h)
-            big(T.V, "V", lab, "lab", T.Lu, "Lu", h)
-            big(T.X, "X", xa, "xa", T.Lu, "Lu", h)
-        hosts(t)
+            step(t, "lu%d" % h)
+            for k in ("Lu", "Lf")[1 - CFG["u16"]:] if t else (): op("x", None, 0.0, "", "%s%d%d" % (k, t, h), "x", "%s%d%d" % (k, t, h), len(lanes(prv, core)))
+            if t and not CFG["u16"]: cp(T["Lu%d" % t][:, H[h]], T["Lf%d" % t][:, H[h]], 128, "Lf%d%d" % (t, h), "Lu%d%d" % (t, h))
+            big(T.V, "V", lab, "lab", T["Lu%d" % t], "Lu%d" % t, h)
+            big(T.X, "X", xa, "xa", T["Lu%d" % t], "Lu%d" % t, h)
+            step(t, "vc%d" % h)
+            for k in range(16): mm(T.VC[:, 8 * h:8 * h + 8, k], xcols(T.V, h, k), T.W8b[:, 24:32], True, True, 64, parts("V", h) + " W8b3", "VC.v%d" % h)
+        for hs in CFG["hs"]: hosts(t, hs)
+        for h in (1, 0): front(t, h)
+        for b in range(15, -1, -1):
+            step(t, "sc%d" % (b // 8))
+            if CFG["join"] and b > 7: put(T.win[:, 0:WN], T.OFF[:, 2 * b:2 * b + 2], T.VAL[:, b, :], 32, "OFFp1 OFFh1 VALj VALp1", "lab don")
+            elif CFG["join"]: put(T.win[:, 0:WN], T.OFF[:, 2 * b:2 * b + 1], T.VAL[:, b, 0:16], 16, "OFFh0 VALp0", "lab don")
+            else: put(T.win[:, DON0:WN], T.OFF[:, 2 * b:2 * b + 1], T.VAL[:, b, 0:16], 16, "OFFh%d VALp%d" % (b // 8, b // 8), "don")
         for h in (1, 0):
-            front(t, h)
-            tag[0] = "sc%d" % h
-            for b in range(8 * h + 7, 8 * h - 1, -1):
-                cp(T.win[:, 0:WN].indirect(T.OFF[:, 2 * b:2 * b + 2]), T.VAL[:, b, :], 32 * CFG["scat"], "OFFp%d OFFh VALj VALp%d" % (h, h), "lab don")
-        if t == ST - 1: dma("s", "d_yb", T.yb[:], T.win[0:128:16, 0:W], 32 * W, "lab", "")
-        for h in (1, 0):
-            tag[0] = "mi%d" % h; pu, d0 = T.pu[:, 8 * h:8 * h + 8], DON0 + (S + 16) * t + 128 * h
-            tt(T.NA[:, H[h]], lab.indirect(pu), T.JR[:, H[h]], A.is_equal, 128 * GA, "lab JR pu%d" % h, "NA%d" % h)
-            tt(T.CD[:, H[h]], T.win[:, d0:d0 + 128], T.NA[:, H[h]], A.mult, 256, "don NA%d" % h, "CD%d" % h)
-            tt(T.CP[:, H[h]], T.nbw[:, 0:W].indirect(pu), T.CD[:, H[h]], A.max, 128 * GA, "nbw pu%d CD%d" % (h, h), "CP%d" % h)
+            step(t, "mi%d" % h); d0 = DON0 + (S + 16) * t + 128 * h
+            tt(T.CP[:, H[h]], T.nbw[:, 0:W].indirect(T.pu[:, 8 * h:8 * h + 8]), T.win[:, d0:d0 + 128], A.max, 128 * GA, "nbw pu%d don" % h, "CP%d" % h)
             cp(T.cu[:, H[h]], T.CP[:, H[h]], 128, "CP%d" % h, "cu%d" % h)
-            act(T.vs[:, H[h]], T.CP[:, H[h]], F.Sign, 128, "CP%d" % h, "vs%d" % h, bias=3)
+            step(t, "vv%d" % h); act(T.vs[:, H[h]], T.CP[:, H[h]], F.Sign, 128, "CP%d" % h, "vs%d" % h, bias=3)
+        step(t, "sl0")
+        for b in range(7 if CFG["join"] else 15, -1, -1): put(T.win[:, 0:DON0], T.OFF[:, 32 + 2 * b:33 + 2 * b], T.VAL[:, b, 16:32], 16, "OFFp%d VALj" % (b // 8), "lab")
+        if t == ST - 1: dma("s", "d_yb", T.yb[:], T.win[0:128:16, 0:W], 32 * W, "lab", "")
         for h in (1, 0): big(T.X, "X", xab, "xa xb", T.cu, "cu", h)
         for h in (1, 0): back(t, h)
-    if "o" not in ORDER: ORDER["o"] = arrange(ops)[1]
-    emit(g, T, [ops[i] for i in ORDER["o"]])
+    ops = lump(ops)
+    if "o" not in ORDER: ORDER["e"], ORDER["o"] = improve(ops, arrange(ops)[1])
+    emit(g, T, [dict(ops[i], e=e) for i, e in ORDER["o"]])

import math
from concourse.mybir import AluOpType, ActivationFunctionType

W, S, ST, HOP = 4608, 256, 3, 1
TRASH = W
DON0 = W + 16
WN = DON0 + ST * (S + 16)
MAGIC = 12582912.0
B23, B24 = 8388608.0, 16777216.0
GS = 16384.0
LS = 1024.0
ISC = {"one": 1.0, "s16": 0.0625, "p8192": 8192.0, "p4608": 4608.0, "n4608": -4608.0, "n2304": -2304.0,
       "p4096": 4096.0, "neg": -1.0, "nB": -B23, "n32": -32.0, "n8192": -8192.0}
ISN = list(ISC)
SCRATCH = {}
for _dt, _list in (
    ("float32", "win:%d lbf:288 thn:128 Lf0:256 Lf1:256 Lf2:256 nw0:256 nw1:256 nw2:256 M:4096 ysb:256 SM:256 tc:256 PW:256 "
                "QS:256 KB:256 KS:256 SM2:256 pd:16 ROF:1024 CF:8x32 Q1:256 L4:256 IG:128 CP:256 t2:256 VAL:16x32 ONE:128 IF:128 BO:128 BT:128 WY:128 B8:16 W8f:24 "
                "JR:256 JM:256 BC:16 cf:48 tg:24 lbo:288" % WN),
    ("bfloat16", "xw:%d X:4096 V:4096 GE:256 EP:256 SB:256 EH:8x16 U:256 R:256 vs:256 TK:256 VS:16x24 EQ:128x16 HD:256 e5:16 HW:16 "
                 "IS:%d W8b:32 RR:256 DM:256 TRI:128 RST:128 RA:128 RB:128 RT:128 RM:256 KC2:16x16 N75:128 CT:256 JW:16 CI:8x32 ROT:1024 CR:1024 "
                 "MG:256 O2:256 lbh:288" % (2 * W, 128 * len(ISC))),
    ("int32", "nbw:%d lbs:288 tri:256 thi:128 HI:16 HJ:16 ci:48 cj:8" % W),
    ("uint16", "Lu0:256 Lu1:256 Lu2:256 nu0:256 nu1:256 cu:256 pu:16 OFF:64 cw:48"),
):
    for _e in _list.split():
        SCRATCH[_e.split(":")[0]] = ("sbuf", [128] + [int(_x) for _x in _e.split(":")[1].split("x")], _dt)
BANKS = {"Y0": [128, 4], "Y1": [128, 4], "K0": [512], "K1": [512], "P0": [512], "P1": [512], "VC": [32, 16], "K2": [32, 16]}
for _b in BANKS: SCRATCH[_b] = ("psum", [128] + BANKS[_b], "float32")
SEMAPHORES = (["cv", "ca", "cp", "cg", "sent", "d_lb", "d_tr", "d_th", "d_xa", "d_xb", "d_nb", "d_lab", "d_yb", "d_yc", "d_y0", "d_y1"]
              + ["%s%d%d" % (k, t, h) for k in ("Lu", "Lf") for t in range(1, ST) for h in range(2)])
A, F = AluOpType, ActivationFunctionType
CFG = {"q": 64, "z": 1152, "gath": 1.55, "scat": 3.5, "fix": 55.0, "ind": 55.0, "pe": 0.47, "pf": 3.0, "cyc": 0.93, "dma": 2400.0, "care": 1000.0, "link": 3600.0, "wake": 45.0, "own": 180.0, "late": 80.0, "lump": 600.0, "seed": 1, "tries": 65000, "heat": 300.0, "flip": 1e9, "rep": 2, "lane": 1, "u16": 0, "seedk": True, "join": False, "gift": "vv", "hs": [(1, 0)], "dd": "vv"}
PLAN = 2 * ["lu1 X1a:a X1b:v y1a y1b V1a:a V1b:v yc1:a yd1:v lu0 M1a M1b V0a:a xs1 M1c M1d vc1 V0b:a vc0 kb1 vs X0a:a eqa eqb ys1:a X0b:a y0a y0b "
            "yc0:a yd0:a ho co1 hd xs0 M0a M0b un1 M0c M0d ys0:a kb0 un0 sc1 sc0 mi1 co0 C1a:a C1b:a mi0 dd1 dd0 sl0 C0a:a pr1 vv1 "
            "N1a N1b N1c N1d rs1 C0b:a fi1 vv0 pr0 rs0 N0a N0b N0c N0d fi0"]
ORDER = {}


def follow(ops):
    pre = [set() for _ in ops]; lastw, readers = {}, {}
    for i, o in enumerate(ops):
        for k in o["r"] + o["w"]:
            if k in lastw: pre[i].add(lastw[k])
        for k in o["w"]: pre[i].update(readers.get(k, []))
        for k in o["r"]: readers.setdefault(k, []).append(i)
        for k in o["w"]:
            lastw[k] = i; readers[k] = []
    return pre


def lump(ops):
    made = set(k for o in ops if o["t"] for k in o["w"]); out = []
    for o in ops:
        p = out[-1] if out else None
        if p and o["e"] == p["e"] == "p" and o["w"] == p["w"] and made & set(o["r"]) <= set(p["r"]) and p["c"] + o["c"] <= CFG["lump"]:
            out[-1] = dict(p, f=lambda q, e, a=p["f"], b=o["f"]: (a(q, e), b(q, e))[1], c=p["c"] + o["c"], r=p["r"] + o["r"], st=p["st"] or o["st"], sp=o["sp"])
        else: out.append(o)
    return out


def graph(ops):
    pre = follow(ops); sent, soft, closed = {}, set(), {}
    for i, o in enumerate(ops):
        if o["e"] == "s":
            if "s" in sent and sent["s"] not in pre[i]: pre[i].add(sent["s"]); soft.add((sent["s"], i))
            sent["s"] = i
        if o["k"] == "r":
            sent[o["sem"]] = i; soft.update((j, i) for j in pre[i] if ops[j]["k"] == "r")
        if o["k"] == "x": pre[i].add(sent[o["sem"]])
        if o["e"] == "p":
            b = o["w"][0].split(".")[0]
            if o["st"] and b in closed: pre[i].add(closed[b])
            if o["sp"]: closed[b] = i
    return pre, soft


def place(ops, order, pre, soft, eng):
    n = len(ops); wake = CFG["wake"]; t0, t1, done = [0.0] * n, [0.0] * n, [0.0] * n; busy = {}; dma = 0.0

    def clash(k, a, b, e):
        l = busy.setdefault(k, []); lo, hi = 0, len(l)
        while lo < hi:
            m = (lo + hi) // 2
            if l[m][0] < b: lo = m + 1
            else: hi = m
        while lo and l[lo - 1][1] > a + 1e-3:
            lo -= 1
            if l[lo][2] != e: return l[lo][1]
        return None
    for i in order:
        o = ops[i]; e = eng[i]; c = o["c"] + (10.0 if e == "a" else 0.0); x = 0.0
        t = max([t1[j] if (j, i) in soft or eng[j] == e == "p" else done[j] + wake for j in pre[i]] + [0.0])
        while x is not None:
            x = clash(e, t, t + c, "")
            if x is not None: t = x
            for b in o["b"] if x is None else []:
                x = clash(b, t - wake, t + c + wake, e)
                if x is not None:
                    t = x + wake; break
        t0[i], t1[i], done[i] = t, t + c, t + c + o["lat"]
        for k in [e] + o["b"]:
            busy[k].append((t, t + c, e)); busy[k].sort()
        if o["k"] == "d":
            dma = max(dma, t1[i] + 1200.0) + o["lat"]; done[i] = dma + 800.0
    return t0, max(done)


def arrange(ops):
    pre, soft = graph(ops); n = len(ops); key = [1e9] * n; eng = [o["e"] for o in ops]
    for i, o in enumerate(ops):
        if o["t"]:
            names = PLAN[min(o["t"][0], 1)].split(); j = [x.split(":")[0] for x in names].index(o["t"][1])
            key[i] = 1000.0 * o["t"][0] + j
            if o["e"] == "va": eng[i] = names[j][-1]
    for i in range(n - 1, -1, -1):
        for j in pre[i]:
            if not ops[j]["t"]: key[j] = min(key[j], key[i])
    key = [k if o["t"] else k * 1e-9 - 2.0 for k, o in zip(key, ops)]
    for i in range(n): key[i] = max([key[i]] + [key[j] for j in pre[i]])
    t0, end = place(ops, sorted(range(n), key=lambda i: (key[i], i)), pre, soft, eng)
    return end, [(i, eng[i]) for i in sorted(range(n), key=lambda i: (t0[i], i))]


def improve(ops, order):
    pre, soft = graph(ops); n = len(ops); own = CFG["own"]; state = [CFG["seed"]]
    seen = {e: CFG["late"] if e == "v" else CFG["wake"] for e in "vapgsx"}
    seq = [i for i, e in order]; eng = [e for i, e in sorted(order)]; flex = [i for i in range(n) if ops[i]["e"] == "va"]
    P = [[(j, (j, i) in soft or ops[j]["e"] == ops[i]["e"] == "p") for j in pre[i]] for i in range(n)]
    C, L, B, D = [o["c"] for o in ops], [o["lat"] for o in ops], [o["b"] for o in ops], [o["k"] == "d" for o in ops]

    def rnd(m):
        state[0] = (state[0] * 1103515245 + 12345) % 2147483648; return (state[0] >> 8) % m

    above = [0] * n
    for i in range(n):
        far = 0
        for j in pre[i]: far |= above[j]
        P[i] = [(j, s) for j, s in P[i] if not far >> j & 1]; above[i] = far | sum(1 << j for j in pre[i])
    others = [{e: [b + x for b in B[i] for x in "vap" if x != e] for e in ops[i]["e"]} for i in range(n)]
    mine = [{e: [e] + [b + e for b in B[i]] for e in ops[i]["e"]} for i in range(n)]

    def clock(seq, a, was):
        t1, near, far, why = was[2][:], was[3][:], was[4][:], was[5][:]; marks = was[6][:a // 32 + 1]
        last, dma, end, top = marks[-1]; last = dict(last)
        for p in range(a - a % 32, n):
            if p % 32 == 0 and p > a: marks.append((dict(last), dma, end, top))
            i = seq[p]; e = eng[i]; w = last.get(e, -1); t = t1[w]
            for j, s in P[i]:
                x = t1[j] if s else near[j] if eng[j] == e else far[j]
                if x > t: t = x; w = j
            for k in others[i][e]:
                j = last.get(k, -1)
                if far[j] > t: t = far[j]; w = j
            t += C[i] + (10.0 if e == "a" else 0.0); t1[i] = t; why[i] = w
            for k in mine[i][e]: last[k] = i
            if D[i] and "labd" in ops[i]["w"]: t += CFG["dma"] + L[i]
            elif D[i]:
                dma = max(dma, t + 0.6 * CFG["dma"]) + L[i]; t = dma + 0.4 * CFG["dma"]
            else: t += L[i]
            near[i] = t + own; far[i] = t + seen[e]
            if t > end: end = t; top = i
        return end, top, t1, near, far, why, marks
    now = clock(seq, 0, (0, 0, [0.0] * (n + 1), [0.0] * (n + 1), [0.0] * (n + 1), [-1] * n, [({}, 0.0, 0.0, 0)])); best = (now[0], seq, list(eng))
    for it in range(CFG["tries"]):
        arcs = []; i = now[1] if rnd(5) else rnd(n); old = None; why = now[5]
        while why[i] >= 0:
            if why[i] not in pre[i]: arcs.append((why[i], i))
            i = why[i]
        if rnd(16) == 0:
            m = flex[rnd(len(flex))]; old = list(eng); eng[m] = "v" if eng[m] == "a" else "a"; new = seq; a = seq.index(m)
        elif not arcs: continue
        else:
            j, i = arcs[rnd(len(arcs))]; a, b = seq.index(j), seq.index(i); far = (0, 0, 0, 2, 5, 15)[rnd(6)]
            if rnd(2):
                a = max(0, a - far); need = set(pre[i]); mv = [i]
                for k in reversed(seq[a:b]):
                    if k in need: need.update(pre[k]); mv.append(k)
                if j in mv: continue
                new = seq[:a] + mv[::-1] + [k for k in seq[a:b] if k not in need] + seq[b + 1:]
            else:
                b = min(n - 1, b + far); s = {j}; mv = [j]
                for k in seq[a + 1:b + 1]:
                    if not s.isdisjoint(pre[k]): s.add(k); mv.append(k)
                if i in s: continue
                new = seq[:a] + [k for k in seq[a:b + 1] if k not in s] + mv + seq[b + 1:]
        r = clock(new, a, now)
        if r[0] <= now[0] - (CFG["heat"] * (1.0 - it / CFG["tries"]) + 1.0) * math.log((rnd(4096) + 1) / 4097.0):
            now = r; seq = new
            if it % 50 == 0:
                seq = sorted(seq, key=lambda i: r[2][i] - C[i]); now = clock(seq, 0, now)
            if now[0] < best[0]: best = (now[0], seq, list(eng))
        elif old: eng[:] = old
    return best[0], [(i, best[2][i]) for i in best[1]]


def emit(g, T, ops):
    Q = {"v": g.vector, "a": g.scalar, "p": g.tensor, "g": g, "s": g.sync}
    deps = follow(ops); bank = {}
    for i, o in enumerate(ops):
        for k in o["b"]:
            deps[i].update(j for e2, j in bank.setdefault(k, {}).items() if e2 != o["e"])
            bank[k][o["e"]] = i
        if o["e"] == "p": deps[i] = set(j for j in deps[i] if ops[j]["e"] != "p")
        if o["k"] == "r": deps[i] = set(j for j in deps[i] if ops[j]["k"] != "r")
    need = set(j for d in deps for j in d)
    tick, n = {}, {}
    for i, o in enumerate(ops):
        if o["k"] == "c" and i in need:
            n[o["e"]] = n.get(o["e"], 0) + 1; tick[i] = ("c" + o["e"], n[o["e"]])
        elif o["k"] in ("d", "x"): tick[i] = (o["sem"], o["n"])
    know = {e: {} for e in Q}; snap = {}
    for i, o in enumerate(ops):
        e = o["e"]
        if o["k"] == "x":
            snap[i] = {}; continue
        kn = know[e]; want = {}
        for j in deps[i]:
            s, v = tick[j]
            if want.get(s, (0, 0))[0] < v: want[s] = (v, j)
        for s, (v, j) in sorted(want.items(), key=lambda z: -z[1][1]):
            if kn.get(s, 0) < v:
                Q[e].wait_ge(T.sem[s], v); kn[s] = v
                for s2, v2 in snap[j].items(): kn[s2] = max(kn.get(s2, 0), v2)
        snap[i] = dict(kn)
        ins = o["f"](Q[e], e)
        if o["k"] == "d": ins.then_inc(T.sem[o["sem"]], 16)
        elif o["k"] == "c" and i in tick: ins.then_inc(T.sem[tick[i][0]], 1)
    top = {}
    for s, v in tick.values(): top[s] = max(top.get(s, 0), v)
    g.wait_ge(T.sem.sent, sum(o["n"] for o in ops if o["k"] == "r"))
    for s, v in top.items():
        if max(kn.get(s, 0) for kn in know.values()) < v: g.sync.wait_ge(T.sem[s], v)


def rank_program(g, core, T, topo):
    rank = T.rank_of(core)
    if rank is None:
        return
    nr = len(T.cores)
    nxt, prv = T.cores[(rank + HOP) % nr], T.cores[(rank - HOP) % nr]
    tag = [None]; ops = []; FX, GA, PE = CFG["fix"], CFG["gath"], CFG["pe"]

    def step(t, name): tag[0] = (t, name)
    def type_of(n): return abs(n - round(n)) > 1e-6 or round(n) in (56, 112)
    def op(e, f, c, r, w, k="c", sem=None, n=0, lat=0.0, st=False, sp=False):
        if k == "c" and e in ("v", "a", "va"): c = (CFG["ind"] if type_of(c - FX) else FX) + (c - FX) * CFG["cyc"]
        banks = sorted(set(x.split(".")[0] for x in (r + " " + w).split()) & set(BANKS))
        ops.append({"e": e, "f": f, "c": c, "r": r.split(), "w": w.split(), "k": k, "sem": sem, "n": n, "lat": lat, "t": tag[0], "st": st, "sp": sp, "b": banks})
    def dma(e, sem, out, in_, nb, r, w): op(e, lambda q, e: q.dma_start(out, in_), 60.0, r, w, "d", sem, 16, nb / 250.0)
    def mm(out, l, rh, st, sp, n, r, w): op("p", lambda q, e: q.matmul(out, l, rh, st, sp), n * PE + CFG["pf"], r, w, st=st, sp=sp)
    def cp(out, in_, n, r, w): op("v", lambda q, e: q.tensor_copy(out, in_), FX + n, r, w)
    def tt(out, a, b, o, n, r, w): op("v", lambda q, e: q.tensor_tensor(out, a, b, o), FX + n, r, w)
    def ts(out, a, s1, o0, n, r, w, s2=None, o1=None):
        if o1 is None: op("v", lambda q, e: q.tensor_scalar(out, a, s1, None, o0), FX + n, r, w)
        else: op("v", lambda q, e: q.tensor_scalar(out, a, s1, s2, o0, o1), FX + n, r, w)
    def scan(out, d0, d1, o0, o1, n, r, w): op("v", lambda q, e: q.tensor_tensor_scan(out, d0, d1, 0.0, o0, o1), FX + n, r, w)
    def ms(ap, c, n, w): op("v", lambda q, e: q.memset(ap, c), FX + n, "", w)
    def act(out, in_, fn, n, r, w, bias=None, scale=1.0, col=None):
        if bias is not None: col, r = T.BC[:, bias:bias + 1], r + " BC%d" % bias
        if col is None: op("a", lambda q, e: q.activation(out, in_, fn, scale=scale), FX + n, r, w)
        else: op("a", lambda q, e: q.activation(out, in_, fn, bias=col, scale=scale), FX + n, r, w)
    def either(out, in_, n, r, w, e="va"):
        op(e, lambda q, e: q.tensor_copy(out, in_) if e == "v" else q.activation(out, in_, F.Copy), FX + n, r, w)
    def put(win, off, val, n, r, w):
        op("v", lambda q, e: q.tensor_scalar(win.indirect(off), val, 1.0, float(W), A.mult, A.add), FX + n * CFG["scat"], r, w, sem="put")
    def iota(out, pat, base, cm, n, w, fl=True):
        if fl: op("g", lambda q, e: q.iota(out, pat, base, cm, allow_small_or_imprecise_dtypes=True), 130.0 + 2 * n, "", w)
        else: op("g", lambda q, e: q.iota(out, pat, base, cm), 130.0 + 2 * n, "", w)
    def sel(out, in_, pat, cmp, fill, base, cm, n, r, w): op("g", lambda q, e: q.affine_select(out, in_, pat, cmp, fill, base, cm), 170.0 + 2 * n, r, w)
    def I(name):
        j = ISN.index(name); return T.IS[:, 128 * j:128 * j + 128]
    def whole(out, stop, w):
        for j in range(2): mm(out, I("one"), T.MG[:, 128 * j:128 * j + 128], False, stop and j == 1, 128, "Ione MG", w)

    H = [slice(0, 128), slice(128, 256)]
    Yb, Kb, Pb = [T.Y0, T.Y1], [T.K0, T.K1], [T.P0, T.P1]
    rcol = T.cf[:, 40:41]; NQ = 128 // CFG["q"]; Z = CFG["z"]

    dma("s", "d_lb", T.lbs[:], T.lb[:], 32 * W, "", "lbs")
    dma("s", "d_tr", T.tri[:], T.tr[:], 131072, "", "tri")
    dma("s", "d_th", T.thi[0:1, :], T.th[:], 512, "", "thi")
    dma("s", "d_xa", T.xw[:, 0:W], T.xs[:], 288 * W, "", "xa")
    iota(T.ONE[:], [[0, 128]], 1, 0, 128, "ONE")
    ms(T.win[:, 0:Z], 0.0, Z, "z0"); ms(T.win[:, Z:W - 2 * Z], 0.0, W - 3 * Z, "z1")
    for j in (2, 1): act(T.win[:, W - j * Z:W - j * Z + Z], T.win[:, 0:Z], F.Copy, Z, "z0", "z%d" % (j + 1))
    cp(T.lbf[:], T.lbs[:], 288, "lbs", "lbf")
    dma("s", "d_lab", T.win[0:128:16, 0:W], T.lbf[:], 32 * W, "lbf", "lab labd z0 z1 z2 z3")
    dma("s", "d_nb", T.nbw[:], T.nb[:], 512 * W, "labd", "nbw")
    dma("s", "d_xb", T.xw[:, W:2 * W], T.xs[:], 256 * W, "", "xb")
    sel(T.IF[:], T.ONE[:], [[-1, 128]], A.is_equal, 0.0, 0, 1, 128, "ONE", "IF")
    sel(T.B8[:, 8:16], T.ONE[:, 0:8], [[-16, 8]], A.is_ge, 0.0, 0, 1, 8, "ONE", "B8t")
    sel(T.B8[:, 0:8], T.B8[:, 8:16], [[16, 8]], A.is_ge, 0.0, 15, -1, 8, "B8t", "B8")
    sel(T.W8f[:, 16:24], T.ONE[:, 0:8], [[-16, 8]], A.is_equal, 0.0, 0, 1, 8, "ONE", "Wself")
    sel(T.BT[:], T.ONE[:], [[-16, 8], [0, 16]], A.is_ge, 0.0, 0, 1, 128, "ONE", "BT")
    sel(T.BO[:], T.BT[:], [[16, 8], [0, 16]], A.is_ge, 0.0, 15, -1, 128, "BT", "BO")
    iota(T.RR[:], [[0, 16], [1, 16]], 0, 0, 256, "RR")
    iota(T.ci[:, 0:16], [[16, 16]], 15, 0, 16, "ci0", False)
    iota(T.ci[:, 16:32], [[1, 16]], 0, 0, 16, "ci1", False)
    iota(T.ci[:, 32:48], [[0, 16]], 0, 1, 16, "ci2", False)
    iota(T.KC2[:], [[0, 16], [-256, 16]], 3840, 0, 256, "KC2")
    iota(T.JR[:], [[1, 256]], 0, 0, 256, "JR")
    iota(T.O2[:], [[0, 256]], 1, 0, 256, "O2")
    sel(T.CI[:], T.O2[:], [[-16, 8], [0, 2], [-1, 16]], A.is_equal, 0.0, 0, 1, 256, "O2", "CI")
    for d in range(8): sel(T.ROT[:, 128 * d:128 * d + 128], T.CI[:, :, d + 1:d + 17], [[-1, 128]], A.not_equal, -1.0, 0, 1, 128, "CI", "ROT%d" % d)
    for d in range(8 if "p" in CFG["dd"] else 0): sel(T.ROF[:, 128 * d:128 * d + 128], T.ROT[:, 128 * d:128 * d + 128], [[0, 128]], A.is_ge, 0.0, 0, 1, 128, "ROT%d" % d, "ROF%d" % d)
    iota(T.VAL[:], [[16, 16], [0, 2], [1, 16]], -W, 0, 512, "VALp0 VALp1 VALj")
    iota(T.win[:, W:WN], [[0, WN - W]], 0, 0, WN - W, "don")
    for nm in ISN: act(I(nm), T.IF[:], F.Copy, 128, "IF", "I" + nm, scale=ISC[nm])
    for j, c in enumerate((-16.0, 16.0, 1.0)): act(T.W8b[:, 8 * j:8 * j + 8], T.B8[:, 0:8], F.Copy, 64, "B8", "W8b%d" % j, scale=c)
    act(T.W8b[:, 24:32], T.W8f[:, 16:24], F.Copy, 64, "Wself", "W8b3")
    for j, c in enumerate((32.0, -32.0)): act(T.W8f[:, 8 * j:8 * j + 8], T.B8[:, 0:8], F.Copy, 64, "B8", "W8f%d" % j, scale=c)
    act(T.WY[:], T.BO[:], F.Copy, 128, "BO", "WY", scale=-16.0 * GS)
    act(T.IG[:], T.IF[:], F.Copy, 128, "IF", "IG", scale=GS)
    cp(T.Lu0[:], T.tri[:], 256, "tri", "Lu00 Lu01")
    ms(T.N75[:], -7.5, 64, "N75")
    ms(T.MG[:, 0:128], MAGIC, 64, "MG"); ms(T.MG[:, 128:256], -MAGIC, 64, "MG")
    cp(T.Lf0[:], T.tri[:], 256, "tri", "Lf00 Lf01")
    ts(T.cj[:, 0:8], T.ci[:, 32:40], 15, A.bitwise_and, 64, "ci2", "cj")
    cp(T.cf[:, 0:40], T.ci[:, 0:40], 64, "ci0 ci1 ci2", "cf")
    cp(T.cw[:, 0:32], T.ci[:, 0:32], 64, "ci0 ci1", "cw")
    cp(T.cf[:, 40:48], T.cj[:, 0:8], 64, "cj", "rcol")
    ts(T.RST[:], T.RR[:, 0:128], 0.0, A.is_equal, 64, "RR", "RST", B24, A.mult)
    ts(T.thn[0:1, :], T.thi[0:1, :], -16.0 * GS, A.mult, 128, "thi", "thn", -15.0 * GS, A.add)
    for j, c in ((0, -8192.0), (1, float(W)), (2, -15.5), (3, -4607.5), (4, 8192.0)): ms(T.BC[:, j:j + 1], c, 64, "BC%d" % j)
    ts(T.BC[:, 5:6], rcol, float(TRASH), A.add, 64, "rcol", "BC5")
    ts(T.BC[:, 6:7], rcol, float(S), A.add, 64, "rcol", "BC6")
    ts(T.TRI[:], T.RR[:, 0:128], rcol, A.is_gt, 64, "RR rcol", "TRI", -8192.0, A.mult)
    ts(T.RM[:], T.RR[:], 0.0, A.not_equal, 128, "RR", "RM")
    ts(T.DM[:], T.RR[:], rcol, A.is_equal, 128, "RR rcol", "DM")
    act(T.RA[:], T.DM[:, 0:128], F.Copy, 128, "DM", "RA", scale=-B24)
    ts(T.RT[:], T.DM[:, 0:128], 8192.0, A.mult, 64, "DM", "RT", 1.0, A.max)
    tt(T.RB[:], T.RT[:], T.RM[:, 0:128], A.mult, 256, "RT RM", "RB")
    ts(T.JW[:], T.cf[:, 0:16], rcol, A.add, 64, "cf rcol", "JW", -15.0, A.add)
    ts(T.tg[:, 0:8], T.cf[:, 17:25], rcol, A.add, 64, "cf rcol", "tg0", 16.0, A.is_lt)
    tt(T.tg[:, 8:16], T.tg[:, 0:8], T.cf[:, 17:25], A.mult, 64, "tg0 cf", "tg1")
    tt(T.tg[:, 16:24], T.tg[:, 8:16], T.cf[:, 32:40], A.add, 64, "tg1 cf", "tg2")
    iota(T.CT[:], [[2304, 2], [0, 128]], -6912, 0, 256, "CT")
    for d in range(8): act(T.CR[:, 128 * d:128 * d + 128], T.JR[:, 0:128], F.Abs, 128, "JR tg2", "CR%d" % d, scale=-1.0, col=T.tg[:, 16 + d:17 + d])
    for d in (0, 4):
        k = " ".join("CR%d" % j for j in range(d, d + 4)); c = T.CR[:, 128 * d:128 * d + 512]
        act(c, c, F.Relu, 512, k, k, bias=4, scale=-8192.0)

    def xcols(buf, h, k, step=16): return buf[:, 2048 * h + k:2048 * (h + 1):step]
    def parts(name, h): return " ".join("%s%d_%d" % (name, h, j) for j in range(NQ))

    def big(out, name, win, wk, off, ok, h):
        q = CFG["q"]
        for j in range(NQ):
            c = 128 * h + q * j; step(t, "%s%d%s" % ("C" if ok == "cu" else name, h, "abcd"[j]))
            either(out[:, 16 * c:16 * (c + q)], win.indirect(off[:, c:c + q]), 16 * q * GA, "%s %s%d" % (wk, ok, h), "%s%d_%d" % (name, h, j))

    def energy(t, h, second, stop):
        kk = "K%d.k" % h; c = 8 * second
        for k in range(16): mm(Kb[h][:, k:128:16], xcols(T.X, h, k), T.W8b[:, c:c + 8], False, False, 64, parts("X", h) + " W8b%d" % second, kk)
        R = CFG["rep"]; n = 16 // R
        for k in range(n):
            m = 2048 * h + 128 * R * k; step(t, "%s%d%s" % ("MN"[second], h, "abcd"[k * R // 4]))
            tt(T.M[:, m:m + 128 * R], xcols(T.X, h, k, n), Yb[h][:, :, 0:R], A.max, 128 * R, parts("X", h) + " Y%d.y0 Y%d.y1 Y%d.y2" % (h, h, h), "M%d_%d" % (h, k))
            for j in range(R):
                mm(Kb[h][:, k + n * j:128:16], T.M[:, m + j:m + 128 * R:R], T.W8f[:, c:c + 8], False, stop and k + j == n + R - 2, 256, "M%d_%d W8f%d" % (h, k, second), kk)

    def front(t, h):
        y, yk, kk, L, Lk = Yb[h][:, :, 0], "Y%d.y0" % h, "K%d.k" % h, T["Lf%d" % t][:, H[h]], "Lf%d%d" % (t, h)
        key, P = Kb[h][:, 0:128], Pb[h]
        step(t, "y%da" % h)
        mm(y, I("s16"), T.N75[:], True, False, 128, "Is16 N75", yk)
        for k in range(16):
            step(t, "y%d%s" % (h, "ab"[k // 8])); mm(y, I("s16"), xcols(T.X, h, k), False, False, 128, parts("X", h), yk)
        whole(y, True, yk)
        step(t, "yc%d" % h)
        if CFG["rep"] > 1: either(Yb[h][:, :, 1], y, 128, yk, "Y%d.y1" % h)
        step(t, "yd%d" % h)
        if CFG["rep"] > 2: either(Yb[h][:, :, 2:4], Yb[h][:, :, 0:2], 256, yk + " Y%d.y1" % h, "Y%d.y2" % h)
        step(t, "ys%d" % h); either(T.ysb[:, H[h]], y, 128, yk, "ysb%d" % h)
        step(t, "xs%d" % h)
        mm(key, I("one"), T.RR[:, 0:128], True, False, 128, "Ione RR", kk)
        mm(P[:, 0:128], T.IF[:], L, True, False, 512, "IF " + Lk, "P%d.a" % h)
        energy(t, h, 0, CFG["seedk"])
        step(t, "kb%d" % h)
        act(T.KB[:, H[h]], key, F.Copy, 128, kk, "KB%d" % h)
        step(t, "co%d" % h)
        scan(T.SM[:, H[h]], T.RST[:], T.KB[:, H[h]], A.add, A.min, 128, "RST KB%d" % h, "SM%d" % h)
        tt(T.GE[:, H[h]], T.SM[:, H[h]].indirect(T.cw[:, 0:8]), T.KB[:, H[h]], A.is_equal, 128 * GA, "SM%d KB%d cw" % (h, h), "GE%d" % h)
        mm(P[:, 0:128], T.GE[:, H[h]], I("p8192"), False, True, 128, "GE%d Ip8192" % h, "P%d.a" % h)
        act(T.tc[:, H[h]], P[:, 0:128], F.Relu, 128, "P%d.a" % h, "tc%d" % h, bias=0)
        mm(P[:, 128:256], I("one"), T.TRI[:], True, False, 128, "Ione TRI", "P%d.b" % h)
        mm(P[:, 128:256], T.BO[:], T.tc[:, H[h]], False, True, 512, "BO tc%d" % h, "P%d.b" % h)
        c8, pw = slice(8 * h, 8 * h + 8), T.PW[:, 128 * h + 15:128 * h + 128:16]
        scan(T.PW[:, H[h]], T.RA[:], P[:, 128:256], A.add, A.max, 128, "RA P%d.b" % h, "PW%d" % h)
        cp(T.pu[:, c8], pw, 64, "PW%d" % h, "pu%d" % h)
        step(t, "dd%d" % h)
        off = T.OFF[:, 17:32:2] if h and CFG["join"] else T.OFF[:, 32 + 16 * h:48 + 16 * h:2]
        if CFG["dd"][h] == "v":
            act(T.QS[:, H[h]], P[:, 128:256], F.Copy, 128, "P%d.b" % h, "QS%d" % h)
            tt(T.EP[:, H[h]], T.PW[:, H[h]].indirect(T.cw[:, 0:8]), T.QS[:, H[h]], A.is_equal, 128 * GA, "PW%d cw QS%d" % (h, h), "EP%d" % h)
            scan(T.SB[:, H[h]], T.RB[:], T.EP[:, H[h]], A.mult, A.add, 64, "RB EP%d" % h, "SB%d" % h)
            tt(T.pd[:, c8], pw, T.SB[:, 128 * h + 15:128 * h + 128:16], A.add, 64, "PW%d SB%d" % (h, h), "pd%d" % h)
            ts(off, T.pd[:, c8], -1.0, A.add, 64, "pd%d BC5" % h, "OFFp%d" % h, T.BC[:, 5:6], A.min)
        else:
            for d in range(8): mm(P[:, 8 * d:8 * d + 8], T.ROF[:, 128 * d:128 * d + 128], pw, True, True, 256, "ROF%d PW%d" % (d, h), "P%d.a" % h)
            ts(T.EP[:, 64 * h:64 * h + 64], P[:, 0:64], 0.0, A.is_equal, 64, "P%d.a" % h, "EP%d" % h)
            mm(P[:, 64:72], T.IF[:], pw, True, False, 256, "IF PW%d" % h, "P%d.a" % h)
            for d in range(8): mm(P[:, 64:72], T.CR[:, 128 * d:128 * d + 128], T.EP[:, 64 * h + 8 * d:64 * h + 8 * d + 8], False, d == 7, 64, "CR%d EP%d" % (d, h), "P%d.a" % h)
            ts(off, P[:, 64:72], T.BC[:, 5:6], A.min, 64, "P%d.a BC5" % h, "OFFp%d" % h)
        step(t, "un%d" % h)
        G, D = T.VC[:, 16 + 8 * h:24 + 8 * h, :], Kb[h][:, 256:384]
        mm(G, T.thn[0:1, :], T.ONE[0:1, :], True, False, 512, "ONE thn", "VC.g%d" % h)
        mm(G, T.WY[:], T.ysb[:, H[h]], False, False, 512, "ysb%d WY" % h, "VC.g%d" % h)
        mm(G, T.KB[:, H[h]], T.IG[:], False, CFG["gift"][h] == "a", 512, "IG KB%d" % h, "VC.g%d" % h)
        if CFG["gift"][h] == "v":
            mm(G, I("n8192"), T.O2[:, 0:128], False, True, 128, "In8192 O2", "VC.g%d" % h)
            tt(T.VAL[:, c8, 0:16], G, L, A.min, 128, "VC.g%d %s" % (h, Lk), "VALp%d" % h)
        else:
            act(T.U[:, H[h]], G, F.Sign, 128, "VC.g%d" % h, "U%d" % h, bias=0)
            mm(D, T.IF[:], L, True, False, 512, "IF " + Lk, "K%d.d" % h)
            mm(D, I("p8192"), T.U[:, H[h]], False, True, 128, "U%d Ip8192" % h, "K%d.d" % h)
            act(T.VAL[:, c8, 0:16], D, F.Identity, 128, "K%d.d" % h, "VALp%d" % h, bias=0)

    def hosts(t, hs):
        a, b = 8 * min(hs), 8 * max(hs) + 8; r = slice(a, b); c = slice(16 * a, 16 * b); m = b - a; s = "" if m == 16 else str(hs[0])
        def ks(*names): return " ".join(x + str(h) for x in names for h in hs)
        step(t, "vs" + s)
        act(T.VS[:, r, 0:16], T.VC[:, r, :], F.Copy, 16 * m, ks("VC.v"), ks("VSa"))
        act(T.VS[:, r, 16:24], T.VC[:, r, 0:8], F.Copy, 8 * m, ks("VC.v"), ks("VSb"))
        mm(T.K2[:, r, :], I("one"), T.KC2[:, r, :], True, False, 16 * m, "Ione KC2", ks("K2.k"))
        mm(T.K2[:, r, :], I("one"), T.VS[:, r, 0:16], False, False, 16 * m, ks("VSa"), ks("K2.k"))
        for d in range(1, 9):
            n = 16 if d < 8 else 8; rows = slice(16 * d - 16 + a, 16 * d - 16 + b); step(t, "eq" + "ab"[d // 5] + s); eq = ks("EQ%d" % d)
            tt(T.EQ[:, rows, 0:n], T.VC[:, r, 0:n], T.VS[:, r, d:d + n], A.is_equal, m * n, ks("VC.v", "VSa", "VSb"), eq)
            mm(T.K2[:, r, 0:16 - d], I("p4096"), T.EQ[:, rows, 0:16 - d], False, d == 8, max(64, m * (16 - d)), "Ip4096 " + eq, ks("K2.k"))
            if d < 8: mm(T.K2[:, r, 0:d], I("p4096"), T.EQ[:, rows, 16 - d:16], False, False, max(64, m * d), eq, ks("K2.k"))
        step(t, "ho" + s)
        act(T.KS[:, c], T.K2[:, r, :], F.Copy, 16 * m, ks("K2.k"), ks("KS"))
        scan(T.SM2[:, c], T.RM[:, c], T.KS[:, c], A.mult, A.max, 16 * m, "RM " + ks("KS"), ks("SM2"))
        cp(T.HI[:, r], T.SM2[:, 16 * a + 15:16 * b:16], 64, ks("SM2"), ks("HI"))
        ts(T.HJ[:, r], T.HI[:, r], 255, A.bitwise_and, 64, ks("HI"), ks("HJ"))
        tt(T.HD[:, c], T.HJ[:, r].indirect(T.cw[:, 16:16 + m]), T.DM[:, c], A.mult, 16 * m * GA, "cw DM " + ks("HJ"), ks("HD"))
        for h in hs: mm(T.K2[:, 17, 8 * h:8 * h + 8], T.HD[:, H[h]], T.W8b[:, 16:24], True, True, 64, "W8b2 " + ks("HD"), ks("K2.h"))
        mm(T.K2[:, 16, r], I("neg"), T.JW[:, r], True, False, 64, "Ineg JW", ks("K2.d"))
        for h in hs: mm(T.K2[:, 16, 8 * h:8 * h + 8], T.HD[:, H[h]], T.W8b[:, 16:24], False, h == hs[-1], 64, ks("HD"), ks("K2.d"))
        step(t, "hd" + s)
        ts(T.e5[:, r], T.K2[:, 16, r], 0.0, A.is_equal, 64, ks("K2.d"), ks("e5"), -256.0, A.mult)
        tt(T.HW[:, r], T.K2[:, 17, r], T.e5[:, r], A.add, 64, ks("K2.h", "e5"), ks("HW"))
        for d in range(8):
            mm(T.K2[:, 20 + d, r], T.ROT[:, 128 * d:128 * d + 128], T.HW[:, r], True, True, 64, "ROT%d " % d + ks("HW"), ks("K2.r"))
        ts(T.EH[:, :, r], T.K2[:, 20:28, r], 0.0, A.is_equal, 8 * m, ks("K2.r"), ks("EH"))
        mm(T.K2[:, 18, r], I("one"), T.HW[:, r], True, False, 64, "Ione " + ks("HW"), ks("K2.o"))
        mm(T.K2[:, 18, r], I("n32"), T.e5[:, r], False, False, 64, "In32 " + ks("e5"), ks("K2.o"))
        for d in range(8): mm(T.K2[:, 18, r], T.CR[:, 128 * d:128 * d + 128], T.EH[:, d, r], False, d == 7, 64, "CR%d " % d + ks("EH"), ks("K2.o"))
        ts(T.OFF[:, 2 * a:2 * b:2], T.K2[:, 18, r], T.BC[:, 6:7], A.min, 64, "BC6 " + ks("K2.o"), ks("OFFh"), float(DON0 * CFG["join"] + (S + 16) * t), A.add)

    def back(t, h):
        b, L, Lk, kk, nw = "P%d.p" % h, T["Lf%d" % t][:, H[h]], "Lf%d%d" % (t, h), "K%d.k" % h, T["nw%d" % t][:, H[h]]
        p1, p2, key = Pb[h][:, 256:384], Pb[h][:, 384:512], Kb[h][:, 0:128]
        step(t, "pr%d" % h)
        if CFG["seedk"]: mm(key, T.IF[:], T.KB[:, H[h]], True, False, 512, "IF KB%d" % h, kk)
        mm(Pb[h][:, 256:512], I("one"), T.CT[:], True, False, 256, "Ione CT", b)
        mm(p2, T.IF[:], L, False, False, 512, "IF " + Lk, b)
        mm(p1, T.IF[:], T.CP[:, H[h]], False, False, 512, "IF CP%d" % h, b)
        mm(p1, I("n2304"), T.vs[:, H[h]], False, False, 128, "In2304 vs%d" % h, b)
        energy(t, h, 1, False)
        step(t, "rs%d" % h)
        tt(T.R[:, H[h]], lab.indirect(T.pu[:, 8 * h:8 * h + 8]), T.JR[:, H[h]], A.is_lt, 128 * GA, "lab JR pu%d" % h, "R%d" % h)
        tt(T.Q1[:, H[h]], T.nbw[:, 0:W].indirect(T.pu[:, 8 * h:8 * h + 8]), T.R[:, H[h]], A.mult, 128 * GA, "nbw pu%d R%d" % (h, h), "Q1%d" % h)
        mm(p2, I("n8192"), T.R[:, H[h]], False, False, 128, "In8192 R%d" % h, b)
        step(t, "fi%d" % h)
        mm(key, T.R[:, H[h]], I("nB"), False, True, 128, "R%d InB" % h, kk)
        act(T.TK[:, H[h]], key, F.Sign, 128, kk, "TK%d" % h, bias=2)
        mm(p2, T.TK[:, H[h]], I("n4608"), False, False, 128, "TK%d In4608" % h, b)
        mm(p1, T.TK[:, H[h]], I("p4608"), False, True, 128, "TK%d Ip4608" % h, b)
        tt(T.t2[:, H[h]], p2, T.Q1[:, H[h]], A.max, 128, b + " Q1%d" % h, "t2%d" % h)
        tt(nw, p1, T.t2[:, H[h]], A.max, 128, b + " t2%d" % h, "nw%d%d" % (t, h))
        if t == ST - 1:
            dma("s", "d_y%d" % h, T.yl[:, H[h]], nw, 65536, "nw%d%d" % (t, h), "")
        else:
            rid, pid = topo.addr(nxt)[0:2]
            if CFG["u16"]: cp(T["nu%d" % t][:, H[h]], nw, 128, "nw%d%d" % (t, h), "nu%d%d" % (t, h))
            for src, dst, lat in (("nu", "Lu", CFG["link"] * 0.8), ("nw", "Lf", CFG["link"]))[1 - CFG["u16"]:]:
                def send(q, e, src=T["%s%d" % (src, t)][:, H[h]], dst=T["%s%d" % (dst, t + 1)][:, H[h]], sem=T.sem["%s%d%d" % (dst, t + 1, h)]):
                    return q.remote_dma(dst, src, sem, T.sem.sent, pid, rid, sum(1 << m for m in lanes(core, nxt)))
                op("g", send, 300.0, "%s%d%d" % (src, t, h), "sent", "r", "%s%d%d" % (dst, t + 1, h), len(lanes(core, nxt)), lat)

    def lanes(a, b): return topo.engines(a, b)[::CFG["lane"]]
    lab, xa, xab = T.win[:, 0:W], T.xw[:, 0:W], T.xw[:, 0:2 * W]
    for t in range(ST):
        for h in (1, 0):
            step(t, "lu%d" % h)
            for k in ("Lu", "Lf")[1 - CFG["u16"]:] if t else (): op("x", None, 0.0, "", "%s%d%d" % (k, t, h), "x", "%s%d%d" % (k, t, h), len(lanes(prv, core)))
            if t and not CFG["u16"]: cp(T["Lu%d" % t][:, H[h]], T["Lf%d" % t][:, H[h]], 128, "Lf%d%d" % (t, h), "Lu%d%d" % (t, h))
            big(T.V, "V", lab, "lab", T["Lu%d" % t], "Lu%d" % t, h)
            big(T.X, "X", xa, "xa", T["Lu%d" % t], "Lu%d" % t, h)
            step(t, "vc%d" % h)
            for k in range(16): mm(T.VC[:, 8 * h:8 * h + 8, k], xcols(T.V, h, k), T.W8b[:, 24:32], True, True, 64, parts("V", h) + " W8b3", "VC.v%d" % h)
        for hs in CFG["hs"]: hosts(t, hs)
        for h in (1, 0): front(t, h)
        for b in range(15, -1, -1):
            step(t, "sc%d" % (b // 8))
            if CFG["join"] and b > 7: put(T.win[:, 0:WN], T.OFF[:, 2 * b:2 * b + 2], T.VAL[:, b, :], 32, "OFFp1 OFFh1 VALj VALp1", "lab don")
            elif CFG["join"]: put(T.win[:, 0:WN], T.OFF[:, 2 * b:2 * b + 1], T.VAL[:, b, 0:16], 16, "OFFh0 VALp0", "lab don")
            else: put(T.win[:, DON0:WN], T.OFF[:, 2 * b:2 * b + 1], T.VAL[:, b, 0:16], 16, "OFFh%d VALp%d" % (b // 8, b // 8), "don")
        for h in (1, 0):
            step(t, "mi%d" % h); d0 = DON0 + (S + 16) * t + 128 * h
            tt(T.CP[:, H[h]], T.nbw[:, 0:W].indirect(T.pu[:, 8 * h:8 * h + 8]), T.win[:, d0:d0 + 128], A.max, 128 * GA, "nbw pu%d don" % h, "CP%d" % h)
            cp(T.cu[:, H[h]], T.CP[:, H[h]], 128, "CP%d" % h, "cu%d" % h)
            step(t, "vv%d" % h); act(T.vs[:, H[h]], T.CP[:, H[h]], F.Sign, 128, "CP%d" % h, "vs%d" % h, bias=3)
        step(t, "sl0")
        for b in range(7 if CFG["join"] else 15, -1, -1): put(T.win[:, 0:DON0], T.OFF[:, 32 + 2 * b:33 + 2 * b], T.VAL[:, b, 16:32], 16, "OFFp%d VALj" % (b // 8), "lab")
        if t == ST - 1: dma("s", "d_yb", T.yb[:], T.win[0:128:16, 0:W], 32 * W, "lab", "")
        for h in (1, 0): big(T.X, "X", xab, "xa xb", T.cu, "cu", h)
        for h in (1, 0): back(t, h)
    ops = lump(ops)
    if "o" not in ORDER: ORDER["e"], ORDER["o"] = improve(ops, arrange(ops)[1])
    emit(g, T, [dict(ops[i], e=e) for i, e in ORDER["o"]])
